import numpy as np, ml_dtypes
CORES = [40,64,80,88,96,104,120,144]
N = 8
import mx_ref
BF = ml_dtypes.bfloat16
def gcols(t, e):
    v = np.concatenate([t.reshape(8, 16, -1, 4), np.zeros((8, 16, 1, 4), BF)], axis=2)
    return np.ascontiguousarray(np.stack([v[g][:, e[g]] for g in range(8)])).reshape(128, -1)
def tile(rs):
    return np.stack(rs, axis=2).reshape(128, -1).astype(BF)
def pick(q, e):
    c = np.concatenate([q[0].reshape(128, -1, 4), np.zeros((128, 1, 4), np.uint8)], axis=1); s = np.concatenate([q[1], np.ones((16, 1), np.uint8)], axis=1)
    return (np.ascontiguousarray(c[:, e].reshape(128, -1)), np.ascontiguousarray(s[:, e]))
def join(*qs):
    return (np.concatenate([q[0] for q in qs], axis=1), np.concatenate([q[1] for q in qs], axis=1))
def put(q, e, v):
    c, s = q[0].reshape(128, -1, 4).copy(), q[1].copy(); c[:, e] = v[0].reshape(128, -1, 4); s[:, e] = v[1]
    return (c.reshape(128, -1), s)
def pk(c, s):
    return (np.ascontiguousarray(c), mx_ref.live(s))
def emit(q):
    return q[0], q[1]
def packed(v, rng):
    q = [mx_ref.quantize(np.ascontiguousarray(v[r])) for r in range(N)]
    return np.stack([a for a, b in q]), np.stack([mx_ref.plane(b, rng) for a, b in q])
def values_of_codes():
    e, c = np.zeros((128, 128, 4), np.float32), np.zeros((128, 2, 4), np.uint8)
    e[np.arange(128), np.arange(128), 0] = 1
    c[:127, :, 0] = np.arange(256).reshape(2, 128).T[:127]
    return mx_ref.matmul(mx_ref.quantize(e.reshape(128, 512).astype(BF)), (c.reshape(128, 8), np.full((16, 2), 127, np.uint8))).T.reshape(-1).astype(np.float64)
CODE_VALUE, SCALE_VALUE = values_of_codes(), 2.0 ** (np.arange(256) - 127.0)
def decode(q):
    return (CODE_VALUE[q[0]].reshape(16, 8, -1, 4) * SCALE_VALUE[q[1]][:, None, :, None] + 0.0).reshape(128, -1).astype(np.float32)
def f(rng, *shape):
    return mx_ref.flush((rng.standard_normal(shape, dtype=np.float32) * np.exp2(rng.integers(-2, 3, shape[:-1] + (1,)))).astype(BF))
def wide(rng, *shape, cols=0):
    v = rng.standard_normal(shape, dtype=np.float32) * np.exp2(rng.integers(-12, 13, shape)).astype(np.float32)
    if cols: v *= np.repeat(np.exp2(rng.integers(-cols, cols + 1, shape[:-2] + (1, shape[-1] // 4))) * (rng.random(shape[:-2] + (1, shape[-1] // 4)) > 0.0625), 4, axis=-1).astype(np.float32)
    return mx_ref.flush(v.astype(BF))
C, R = 448, 2
def order(p):
    return np.argsort(-(p[::16] + np.float32(0.0)), axis=1, kind="stable")
def clear(v):
    v = np.array(v)
    v[np.abs(v.astype(np.float32)) < np.float32(2.0 ** -16)] = 0
    return v
def numbers_of(rng):
    return {"x": clear(f(rng, N, 128, 4 * C)), "u": np.array(f(rng, N, 128, 512)), "v": np.array(f(rng, N, 128, 512))}
def weights(rng, w):
    c, p = packed(np.stack([w] * N), rng)
    return {"wc": c, "ws": p}
def aside(rng, k):
    w = np.array(f(rng, 128, 2048)).reshape(8, 16, 4, 8, 16, 4)
    w[:, :k] = 0
    w[:, :, :, :, 0] = 0
    w[:, :, :, :, 8:] = 0
    return weights(rng, w.reshape(128, 2048))
def signs(rng):
    return np.stack([rng.permutation(8) % 2 * 2.0 - 1.0 for r in range(N)])
def setup_inputs(rng):
    return {**numbers_of(rng), **weights(rng, f(rng, 128, 2048))}
def setup_inputs_ties(rng):
    d = numbers_of(rng)
    e = rng.permutation(N)
    x = d["x"].reshape(N, 8, 16, C, 4)
    for r in range(N):
        k = np.zeros(C, int) if r == e[0] else rng.permutation(C) % 3
        a = x[r][:, :8, :3].copy()
        a[:, :, 2] = 0
        x[r][:, :8] = a[:, :, k]
    x[e[1]] = 0
    u = d["u"].reshape(N, 8, 16, 128, 4)
    u[:, :, 8:, ::16] = 0
    w = np.array(f(rng, 128, 2048)).reshape(8, 16, 4, 8, 16, 4)
    w[:, 8:, :, :, :8] = 0
    return {"x": x.reshape(N, 128, 4 * C), "u": u.reshape(N, 128, 512), "v": d["v"], **weights(rng, w.reshape(128, 2048))}
def setup_inputs_near(rng):
    d = numbers_of(rng)
    x = d["x"].astype(np.float32).reshape(N, 8, 16, C, 4)
    s = (np.arange(C) // 2 + rng.integers(0, C // 2, (N, 8, 1))) % (C // 2)
    g = ((s[..., None] >> np.arange(8)) & 1) * np.exp2(np.arange(8) - 23.0)
    x[:, :, 0] = 0
    x[:, :, 0, :, 0] = signs(rng)[:, :, None]
    x[:, :, 8] = g[..., :4]
    x[:, :, 9] = g[..., 4:]
    x[:, :, 10:] = 0
    u = d["u"].reshape(N, 128, 128, 4)
    u[:, :, ::16] = 0
    k = np.where(rng.permutation(N) < N // 2, 2.0 ** -30, 1.0).astype(np.float32).astype(BF)
    for h in range(0, 128, 16):
        u[:, h, h, 0] = k
        u[:, h + 8:h + 10, h] = k[:, None, None]
    return {"x": x.reshape(N, 128, 4 * C).astype(BF), "u": u.reshape(N, 128, 512), "v": d["v"], **aside(rng, 0)}
def setup_inputs_huge(rng):
    d = numbers_of(rng)
    x = 2.0 ** 30 * (0.6 + 0.4 * rng.random((N, 128, C, 4)))
    c = np.stack([rng.permutation(C) % 2 * 2.0 - 1.0 for r in range(N)])
    c[rng.permutation(N) < N // 2] = 1
    x *= c[:, None, :, None]
    u = d["u"].reshape(N, 128, 128, 4)
    a = 2.0 ** 30 * (1 - 0.25 * rng.random((N, 128, 8, 4))) * signs(rng)[:, None, :, None]
    u[:, :, ::16] = a.astype(np.float32).astype(BF)
    w = np.zeros((128, 4, 128, 4), np.float32)
    i = np.arange(128)
    for b in range(4): w[i, b, i, b] = 16
    return {"x": x.astype(np.float32).reshape(N, 128, 4 * C).astype(BF), "u": u.reshape(N, 128, 512), "v": d["v"], **weights(rng, w.reshape(128, 2048).astype(BF))}
def setup_inputs_crowd(rng):
    d = numbers_of(rng)
    x = d["x"].astype(np.float32).reshape(N, 8, 16, C, 4)
    a, b = np.triu_indices(N, 1)
    k = rng.permutation(len(a))[(np.arange(C)[None, :] + np.arange(8)[:, None]) % len(a)]
    z = rng.integers(4, 8, (8, 8, C, 4)) * rng.choice([-1.0, 1.0], (8, 8, C, 4)) * 2.0 ** 26
    s = C - 1 - np.arange(C)
    digits = np.stack([s % 8, s // 8 % 8, s // 64, 0 * s], axis=1)
    for r in range(N):
        l = rng.integers(4, 8, (8, 8, C, 4)) * rng.choice([-1.0, 1.0], (8, 8, C, 4))
        l = np.where((a[k] == r)[:, None, :, None], z, np.where((b[k] == r)[:, None, :, None], -z, l))
        for g in range(8):
            o = rng.permutation(C)
            p = x[r, g]
            p[8:, o] = l[g]
            p[0, o] = digits
    u = d["u"].reshape(N, 128, 128, 4)
    u[:, :, ::16] = 0
    for h in range(0, 128, 16): u[:, h, h, :3] = np.array([1, 8, 64], np.float32).astype(BF)
    return {"x": x.reshape(N, 128, 4 * C).astype(BF), "u": u.reshape(N, 128, 512), "v": d["v"], **aside(rng, 8)}
def setup_inputs_spread(rng):
    d = setup_inputs(rng)
    d["x"] = clear(wide(rng, N, 128, 4 * C, cols=6))
    return d
def check_inputs(d):
    b = []
    for k in ("x", "u", "v"):
        a = np.abs(d[k].astype(np.float32))
        if not (np.isfinite(a).all() and ((a == 0) | (a >= 2.0 ** -30) & (a <= 2.0 ** 30)).all()): b.append("a value of " + k)
    if (d["wc"] != d["wc"][:1]).any(): b.append("wc differs between ranks")
    s = [mx_ref.live(p) for p in d["ws"]]
    if any((p != s[0]).any() for p in s): b.append("ws differs between ranks")
    if not (np.abs(decode(pk(d["wc"][0], d["ws"][0]))) <= 2.0 ** 30).all(): b.append("a number of W beyond 2**30")
    return b
def reference(x, u, v, wc, ws):
    w = pk(wc[0], ws[0])
    lay = [pick(w, np.arange(128 * b, 128 * b + 128)) for b in range(4)]
    qu = [mx_ref.quantize(u[r]) for r in range(N)]
    now = [x[r] for r in range(N)]
    for t in range(R):
        o = [order(mx_ref.matmul(qu[r], mx_ref.quantize(now[r]))) for r in range(N)]
        total = decode(mx_ref.quantize(gcols(now[0], o[0])))
        for r in range(1, N): total = total + decode(mx_ref.quantize(gcols(now[r], o[r])))
        m = mx_ref.quantize((total * np.float32(0.125)).astype(BF))
        h = mx_ref.quantize(tile([np.maximum(mx_ref.matmul(lay[b], m), np.float32(0.0)) * np.float32(0.0625) for b in range(4)]))
        back = decode(h).astype(BF)
        for r in range(N):
            i = np.argsort(o[r], axis=1)
            now[r] = ((now[r].astype(np.float32) + gcols(back, i).astype(np.float32)) * np.float32(0.5)).astype(BF)
    y, ol = np.zeros((N, 128, C), np.float32), np.zeros((N, 8, C), np.float32)
    oc, osc = np.zeros((N, 128, 4 * C), np.uint8), np.zeros((N, 16, C), np.uint8)
    for r in range(N):
        q = mx_ref.quantize(now[r])
        y[r] = mx_ref.matmul(mx_ref.quantize(v[r]), q)
        ol[r] = o[r]
        oc[r], osc[r] = emit(q)
    return {"y": y, "ol": ol, "oc": oc, "osc": osc}

@@ -1,0 +1,431 @@
+from concourse.bass import DstId, RemoteDMATransfer
+from concourse.mybir import dt, AluOpType, ActivationFunctionType
+
+C, R, N = 448, 2, 8
+PC = C // N
+HF = C // 2
+NS = C // 16
+HI, LO = 6, 20
+PAD = 128 - PC
+SW = 464
+X4, U8, BF, F32 = "float8_e4m3fn_x4", "uint8", "bfloat16", "float32"
+
+SCRATCH = {
+    "ps": ("psum", [128, 4096], F32),
+    "ut": ("sbuf", [128, 512], BF), "vt": ("sbuf", [128, 512], BF),
+    "qu": ("sbuf", [128, 128], X4), "su": ("sbuf", [128, 128], U8),
+    "qp": ("sbuf", [128, 128], X4), "sp": ("sbuf", [128, 128], U8),
+    "qv": ("sbuf", [128, 128], X4), "sv": ("sbuf", [128, 128], U8),
+    "qw": ("sbuf", [128, 512], X4), "sw": ("sbuf", [128, 512], U8),
+    "eighth": ("sbuf", [128, 512], BF), "ft": ("sbuf", [128, 2048], BF), "et": ("sbuf", [128, 2048], BF),
+    "qf": ("sbuf", [128, 512], X4), "sf": ("sbuf", [128, 512], U8),
+    "qe": ("sbuf", [128, 512], X4), "se": ("sbuf", [128, 512], U8),
+    "pi": ("sbuf", [128, 8], "int32"), "pf": ("sbuf", [128, 12], F32),
+    "ui": ("sbuf", [128, 8], "int32"), "uo": ("sbuf", [128, 8], "uint16"), "oo": ("sbuf", [128, 8], "uint16"),
+    "t16": ("sbuf", [128, C], BF), "jv": ("sbuf", [128, C], BF),
+    "hot": ("sbuf", [128, C], BF), "keep": ("sbuf", [128, C], BF),
+    "k4": ("sbuf", [128, 12], F32), "k2": ("sbuf", [128, C], BF),
+    "msk": ("sbuf", [128, C], F32), "fill": ("sbuf", [128, C], F32),
+    "eq": ("sbuf", [128, C], BF), "nc": ("sbuf", [128, C], BF),
+    "fl": ("sbuf", [128, 4 * C], BF), "so": ("sbuf", [128, (LO - HI) * HF], "float16"),
+    "sg": ("sbuf", [128, (HI + NS - LO) * SW], BF), "ac": ("sbuf", [128, 16], F32),
+    "iu": ("sbuf", [128, NS], "uint16"), "ob": ("sbuf", [128, C], BF), "ox": ("sbuf", [128, C], "float16"),
+    "ou": ("sbuf", [128, C // 4], "uint16"), "olf": ("sbuf", [128, C], F32),
+    "st": ("sbuf", [128, 4 * C], BF), "acc": ("sbuf", [128, 3 * PC], F32),
+    "mt": ("sbuf", [128, 512], BF), "qm": ("sbuf", [128, 128], X4), "sm": ("sbuf", [128, 128], U8),
+    "ht": ("sbuf", [128, 512], BF), "sn": ("sbuf", [128, 4 * C], F32), "yt": ("sbuf", [128, C], F32),
+}
+SEMAPHORES = ["cv", "cs", "cp", "cg", "du", "dxa", "dxb", "dw", "dv", "dout", "sent"]
+for _t in range(R + 1):
+    SCRATCH["x%d" % _t] = ("sbuf", [128, 4 * C], BF)
+    SCRATCH["qx%d" % _t] = ("sbuf", [128, C], X4)
+    SCRATCH["sx%d" % _t] = ("sbuf", [128, C], U8)
+for _t in range(R):
+    for _n, _w in (("s", C), ("l", C + PAD), ("g", C + PAD), ("r", 2 * PC), ("a", PC)):
+        SCRATCH["q%s_%d" % (_n, _t)] = ("sbuf", [128, _w], X4)
+        SCRATCH["s%s_%d" % (_n, _t)] = ("sbuf", [128, _w], U8)
+    SEMAPHORES += [_s + str(_t) for _s in ("ra", "rb", "ga", "gb", "hr", "ha")]
+
+
+def _bits(engines):
+    return sum(1 << e for e in engines)
+
+
+def _layout(T, topo):
+    cores = list(T.cores)
+    near0 = [r for r in range(N) if r == 0 or topo.may_write(cores[0], cores[r])]
+    order = near0 + [r for r in range(N) if r not in near0]
+    assert len(near0) == N // 2
+    helpers = {}
+    for k, r in enumerate(order):
+        c = cores[r]
+        far = [cores[order[j]] for j in range(N) if j // 4 != k // 4]
+        cand = [h for h in topo.cores_of(c) if h != c and all(topo.may_write(h, d) for d in far)]
+        same = [h for h in cand if topo.die(h) == topo.die(c)]
+        other = [h for h in cand if topo.die(h) != topo.die(c)]
+        helpers[r] = (other[:2], same[:2])
+    return cores, order, helpers
+
+
+def _xfer(topo, src, pairs, in_ap, engines, sem):
+    ids = []
+    for d, _ in pairs:
+        rid, pid = topo.addr(d, src)
+        ids.append(DstId(rid=rid, pnc=pid))
+    if len(pairs) == 1:
+        return RemoteDMATransfer(dst_ids=ids, dma_engine_mask=_bits(engines), remote_sem=sem, src=in_ap, dst=pairs[0][1])
+    return RemoteDMATransfer(dst_ids=ids, dma_engine_mask=_bits(engines), remote_sem=sem, srcs=[in_ap],
+                             dsts=[a for _, a in pairs])
+
+
+def _slot(k, j):
+    return PAD + PC * ((k - j) % 4 if k // 4 == j // 4 else 4 + k % 4)
+
+
+def _view(T, kind, name, a, b):
+    if kind == 0:
+        return T["q" + name][:, a:b].bitcast(dt.uint8)
+    return T["s" + name][:, a:b]
+
+
+def _helper(g, core, T, topo, cores, order, r, kind, i):
+    k = order.index(r)
+    far = [j for j in range(N) if j // 4 != k // 4][2 * i:2 * i + 2]
+    sent = 0
+    for t in range(R):
+        for src, wait, land, sem in (("r_%d", "hr", "l_%d", "rb"), ("a_%d", "ha", "g_%d", "gb")):
+            g.wait_ge(T.sem[wait + str(t)], 8)
+            xs = []
+            for n, j in enumerate(far):
+                d = cores[order[j]]
+                e = topo.engines(core, d)
+                half = len(e) // 2
+                a = n * PC if wait == "hr" else 0
+                xs.append(_xfer(topo, core, [(d, _view(T, kind, land % t, _slot(k, j), _slot(k, j) + PC))],
+                                _view(T, kind, src % t, a, a + PC), e[n * half:(n + 1) * half], T.sem[sem + str(t)]))
+                sent += half
+            g.remote_dma_fused(xs, local_sem=T.sem.sent)
+    g.wait_ge(T.sem.sent, sent)
+
+
+def rank_program(g, core, T, topo):
+    cores, order, helpers = _layout(T, topo)
+    rank = T.rank_of(core)
+    if rank is None:
+        for r in range(N):
+            for kind in (0, 1):
+                if core in helpers[r][kind]:
+                    _helper(g, core, T, topo, cores, order, r, kind, helpers[r][kind].index(core))
+        return
+
+    A, F = AluOpType, ActivationFunctionType
+    V, S, P, Y = g.vector, g.scalar, g.tensor, g.sync
+    Q = {"V": V, "S": S, "P": P, "G": g, "Y": Y}
+    CNT = {"V": "cv", "S": "cs", "P": "cp", "G": "cg"}
+    known = {q: {} for q in Q}
+    total, waited, wr, rd = {}, {}, {}, {}
+
+    def need(q, reads, writes, chain=False):
+        evs = []
+        for key in reads:
+            evs += wr.get(key, [])
+            if key[0] == "B":
+                evs += [e for e in rd.get(key, []) if e[3] != q]
+        for key in writes:
+            evs += [e for e in wr.get(key, []) if not (chain and e[3] == q)] + rd.get(key, [])
+        for sem, val, snap, _ in sorted(evs, key=lambda e: -e[1]):
+            if known[q].get(sem, 0) < val:
+                Q[q].wait_ge(T.sem[sem], val)
+                waited[sem] = max(waited.get(sem, 0), val)
+                known[q][sem] = val
+            for s2, v2 in snap.items():
+                if known[q].get(s2, 0) < v2:
+                    known[q][s2] = v2
+
+    def done(q, sem, n, reads, writes, tag):
+        total[sem] = total.get(sem, 0) + n
+        ev = (sem, total[sem], dict(known[q]), tag)
+        for key in reads:
+            rd.setdefault(key, []).append(ev)
+        for key in writes:
+            wr[key], rd[key] = [ev], []
+
+    def op(q, fn, reads, writes, chain=False):
+        need(q, reads, writes, chain)
+        fn().then_inc(T.sem[CNT[q]], 1)
+        done(q, CNT[q], 1, reads, writes, q)
+
+    def dma(q, sem, pairs, reads, writes):
+        need(q, reads, writes)
+        for o, i in pairs:
+            Q[q].dma_start(o, i).then_inc(T.sem[sem], 16)
+        done(q, sem, 16 * len(pairs), [], writes, "D")
+
+    def arrives(key, sem, n):
+        total[sem] = n
+        wr.setdefault(key, []).append((sem, n, {}, "D"))
+
+    def send(xs, n, reads):
+        need("G", reads, [])
+        g.remote_dma_fused(xs, local_sem=T.sem.sent)
+        total["sent"] = total.get("sent", 0) + n
+
+    def bank(b, a, z):
+        return T.ps[:, 512 * b + a:512 * b + z]
+
+    def mm(b, lq, ls, l0, name, a, n, reads, start=True, stop=True):
+        op("P", lambda: P.matmul_mx(bank(b, 0, n), lq[:, l0:l0 + 128], ls[:, l0:l0 + 128], T["q" + name][:, a:a + n],
+                                    T["s" + name][:, a:a + n], start, stop), reads, ["B%d" % b], chain=not start)
+
+    def quant(name, a, n, tile, reads, writes):
+        op("V", lambda: V.quantize_mx(T["q" + name][:, a:a + n], T["s" + name][:, a:a + n], tile[:, 4 * a:4 * (a + n)]),
+           reads, writes)
+
+    def ts(out, in0, s1, s2, o0, o1, reads, writes):
+        if o1 is None:
+            op("V", lambda: V.tensor_scalar(out, in0, s1, None, o0), reads, writes)
+        else:
+            op("V", lambda: V.tensor_scalar(out, in0, s1, s2, o0, o1), reads, writes)
+
+    me = order.index(rank)
+    mine, cross = me // 4, 1 - me // 4
+    peers = [4 * mine + (me + d) % 4 for d in (1, 2, 3)]
+    on = topo.engines(core, helpers[rank][0][0])
+    off = topo.engines(core, cores[order[peers[0]]])
+    rest = [e for e in on if e not in off]
+
+    dma("S", "du", [(T.ut[:], T.u[:])], [], ["ut"])
+    dma("Y", "dxa", [(T.x0[:, 0:4 * HF], T.x[:, 0:4 * HF])], [], ["x0h0"])
+    dma("Y", "dxb", [(T.x0[:, 4 * HF:4 * C], T.x[:, 4 * HF:4 * C])], [], ["x0h1"])
+    op("G", lambda: g.iota(T.pi[:, 0:1], [[0, 1]], 0, 1), [], ["pi0"])
+    op("G", lambda: g.iota(T.ui[:], [[16, 8]], 0, 0), [], ["ui"])
+    small = dict(allow_small_or_imprecise_dtypes=True)
+    op("G", lambda: g.iota(T.t16[:], [[0, NS], [1, 16]], 0, 0, **small), [], ["t16"])
+    op("G", lambda: g.iota(T.jv[:], [[1, C]], -HF, 0, **small), [], ["jv"])
+    op("V", lambda: V.memset(T.eighth[:], 0.125), [], ["eighth"])
+    op("V", lambda: V.memset(T.ob[:], 0.0), [], ["ob"])
+    ts(T.pi[:, 1:2], T.pi[:, 0:1], 15, None, A.bitwise_and, None, ["pi0"], ["pi1"])
+    ts(T.pi[:, 2:3], T.pi[:, 0:1], 2, 3, A.logical_shift_right, A.bitwise_and, ["pi0"], ["pi2"])
+    ts(T.pi[:, 3:4], T.pi[:, 0:1], 3, None, A.bitwise_and, None, ["pi0"], ["pi3"])
+    op("V", lambda: V.tensor_copy(T.uo[:], T.ui[:]), ["ui"], ["uo"])
+    op("V", lambda: V.tensor_copy(T.pf[:, 0:4], T.pi[:, 0:4]), ["pi0", "pi1", "pi2", "pi3"], ["pf"])
+    ts(T.pf[:, 4:5], T.pf[:, 2:3], 0.0, 4.0, A.is_equal, A.mult, ["pf"], ["pf4"])
+    ts(T.pf[:, 8:9], T.pf[:, 1:2], float(PC * (me % 4) - PAD), None, A.add, None, ["pf"], ["pf8"])
+    ts(T.pf[:, 5:6], T.pf[:, 4:5], T.pf[:, 2:3], -1.0, A.add, A.add, ["pf", "pf4"], ["pf5"])
+    ts(T.pf[:, 6:7], T.pf[:, 4:5], 2.0 * C, T.pf[:, 3:4], A.mult, A.add, ["pf", "pf4"], ["pf6"])
+    ts(T.oo[:], T.ui[:], T.pf[:, 8:9], 0.0, A.add, A.max, ["ui", "pf8"], ["oo"])
+    ts(T.pf[:, 7:8], T.pf[:, 6:7], -4.0 * HF, None, A.add, None, ["pf6"], ["pf7"])
+    ts(T.k4[:, 0:4], T.t16[:, 0:4], T.pf[:, 2:3], 1.0 * C, A.is_equal, A.mult, ["pf", "t16"], ["ka"])
+    ts(T.k4[:, 4:8], T.t16[:, 0:4], T.pf[:, 5:6], -2.0 * C, A.is_equal, A.mult, ["pf5", "t16"], ["kb"])
+    ts(T.hot[:], T.t16[:], T.pf[:, 1:2], None, A.is_equal, None, ["pf", "t16"], ["hot"])
+    op("V", lambda: V.tensor_tensor(T.k4[:, 8:12], T.k4[:, 0:4], T.k4[:, 4:8], A.add), ["ka", "kb"], ["k4"])
+    ts(T.keep[:], T.t16[:], T.pf[:, 1:2], None, A.not_equal, None, ["pf", "t16"], ["keep"])
+    quant("u", 0, 128, T.ut, ["ut"], ["qu"])
+    for b in range(2):
+        ts(T.k2[:, b:C:4], T.t16[:, 0:C // 4], 0.0, T.k4[:, 8 + b:9 + b], A.mult, A.add, ["k4", "t16"], ["k2%d" % b])
+    op("V", lambda: V.tensor_copy(T.qp[:].bitcast(dt.uint32), T.qu[:].bitcast(dt.uint32).indirect(T.uo[:, 0:8])),
+       ["qu", "uo"], ["qp"])
+    op("S", lambda: S.activation(T.sp[:], T.su[:].indirect(T.uo[:, 0:8]), F.Copy), ["qu", "uo"], ["sp"])
+    for b in range(2, 4):
+        ts(T.k2[:, b:C:4], T.t16[:, 0:C // 4], 0.0, T.k4[:, 8 + b:9 + b], A.mult, A.add, ["k4", "t16"], ["k2%d" % b])
+    for b in range(4):
+        op("G", lambda: g.affine_select(T.ft[:, 512 * b:512 * b + 512], T.eighth[:], [[-1, 512]], A.is_equal, 0.0, b, 4),
+           ["eighth"], ["ft%d" % b])
+    for h in range(2):
+        quant("x0", HF * h, HF, T.x0, ["x0h%d" % h], ["qx0h%d" % h])
+    dma("Y", "dw", [(T.qw[:].bitcast(dt.uint8), T.wc[:]), (T.sw[:], T.ws[:])], ["x0h1"], ["qw"])
+    dma("Y", "dv", [(T.vt[:], T.v[:])], [], ["vt"])
+
+    for t in range(R):
+        xk, xn = "x%d" % t, "x%d" % (t + 1)
+        xkeys = [xk + "h0", xk + "h1"] if t == 0 else [xk + "_%d%d" % (b, h) for b in range(4) for h in range(2)]
+        for b in range(2):
+            mm(b, T.qp, T.sp, 0, xk, 0, C, ["qp", "sp", "q" + xk + "h0", "q" + xk + "h1"])
+        cuts = ((0, 128), (128, C))
+        for n, (a, z) in enumerate(cuts):
+            op("V", lambda: V.tensor_tensor(T.msk[:, a:z], bank(0, a, z), T.hot[:, a:z], A.mult), ["B0", "hot"], ["msk%d" % n])
+            op("V", lambda: V.tensor_tensor_scan(T.fill[:, a:z], T.keep[:, a:z], T.msk[:, a:z], 0.0, A.mult, A.add),
+               ["keep", "msk%d" % n], ["fill%d" % n])
+
+        def zc(s):
+            return T.fill[:, 16 * s + 15:16 * s + 16]
+
+        def zk(s):
+            return "fill0" if s < 8 else "fill1"
+
+        outer = list(range(HI)) + list(range(LO, NS))
+        for n, s in enumerate(outer):
+            a, z = (16 * s + 16, C) if s < HI else (0, 16 * s + 16)
+            op("S", lambda: S.activation(T.sg[:, n * SW + a:n * SW + z], bank(1, a, z), F.Sign, bias=zc(s), scale=-1.0),
+               ["B1", zk(s)], ["sga%d" % n])
+        op("V", lambda: V.tensor_tensor(T.eq[:], bank(0, 0, C), T.fill[:], A.is_equal), ["B0", "fill0", "fill1"], ["eq"])
+        for n, s in enumerate(outer):
+            if s < HI:
+                ts(T.sg[:, n * SW:n * SW + 16 * s + 16], bank(0, 0, 16 * s + 16), zc(s), -1.0, A.is_ge, A.mult,
+                   ["B0", zk(s)], ["sgb%d" % n])
+            if n == 0:
+                op("V", lambda: V.tensor_tensor_scan(T.nc[:], T.keep[:], T.eq[:], 0.0, A.mult, A.subtract), ["keep", "eq"], ["nc"])
+            if LO <= s < NS - 1:
+                ts(T.sg[:, n * SW + 16 * s + 16:n * SW + C], bank(0, 16 * s + 16, C), zc(s), None, A.is_le, None,
+                   ["B0", zk(s)], ["sgb%d" % n])
+        ts(T.sg[:, C:HI * SW:SW], T.nc[:, 15:16 * HI:16], -1.0, -16.0, A.mult, A.add, ["nc"], ["sgc0"])
+        ts(T.sg[:, HI * SW + C:len(outer) * SW:SW], T.nc[:, 16 * LO + 15:C:16], -1.0, None, A.mult, None, ["nc"], ["sgc1"])
+        for n, s in enumerate(outer):
+            row = T.sg[:, n * SW:n * SW + C + 1]
+            c = "sgc0" if s < HI else "sgc1"
+            op("S", lambda: S.activation(row, row, F.Relu, scale=-1.0 if s < HI else 1.0, accum_out=T.ac[:, n:n + 1]),
+               [c], ["sga%d" % n, "sgb%d" % n, "ac%d" % n])
+
+        def scan(s):
+            f = (s % 4) * C
+            op("V", lambda: V.tensor_tensor_scan(T.so[:, (s - HI) * HF:(s - HI + 1) * HF], T.fl[:, f:f + HF], T.fl[:, f + HF:f + C],
+                                                 T.nc[:, 16 * s + 15:16 * s + 16], A.add, A.add),
+               ["fa%d" % (s % 4), "fb%d" % (s % 4), "nc"], ["so%d" % s])
+
+        for s in range(HI, LO):
+            f, m = (s % 4) * C, 16 * s + 16
+            ts(T.fl[:, f:f + m], bank(0, 0, m), zc(s), None, A.is_ge, None, ["B0", zk(s)], ["fa%d" % (s % 4)])
+            ts(T.fl[:, f + m:f + C], bank(0, m, C), zc(s), None, A.is_gt, None, ["B0", zk(s)], ["fb%d" % (s % 4)])
+            if s > HI:
+                scan(s - 1)
+        ts(T.iu[:, 0:HI], T.ac[:, 0:HI], -16.0, None, A.add, None, ["ac%d" % n for n in range(HI)], ["iu0"])
+        scan(LO - 1)
+        op("V", lambda: V.tensor_copy(T.iu[:, HI:LO], T.so[:, HF - 1:(LO - HI) * HF:HF]), ["so%d" % s for s in range(HI, LO)], ["iu1"])
+        op("V", lambda: V.tensor_copy(T.ob[:, 0:C].indirect(T.iu[:, 0:LO]), T.jv[:, 0:16 * LO]), ["iu0", "iu1", "jv"], ["ob"])
+        ts(T.iu[:, LO:NS], T.ac[:, HI:len(outer)], -1.0, 1.0 * C, A.mult, A.add, ["ac%d" % n for n in range(HI, len(outer))], ["iu2"])
+        op("V", lambda: V.tensor_copy(T.ob[:, 0:C].indirect(T.iu[:, LO:NS]), T.jv[:, 16 * LO:C]), ["iu2", "jv"], ["ob"])
+        op("V", lambda: V.tensor_tensor_scan(T.ox[:], T.ob[:], T.k2[:], -1000.0, A.max, A.add),
+           ["ob", "k20", "k21", "k22", "k23"], ["ox"])
+        ts(T.ou[:], T.ox[:, 3:C:4], 4.0, T.pf[:, 7:8], A.mult, A.add, ["ox", "pf7"], ["ou"])
+
+        X = T[xk]
+        sk, lk, gk, rk, ak = ["%s_%d" % (n, t) for n in "slgra"]
+        for h, cut in ((cross, 28), (mine, 22)):
+            o0 = PC * h
+            op("S", lambda: S.activation(T.st[:, 16 * (o0 + cut):16 * (o0 + PC)], X[:, 0:4 * C].indirect(T.ou[:, o0 + cut:o0 + PC]), F.Copy),
+               ["ou"] + xkeys, ["stb%d" % h])
+            op("V", lambda: V.tensor_copy(T.st[:, 16 * o0:16 * (o0 + cut)], X[:, 0:4 * C].indirect(T.ou[:, o0:o0 + cut])),
+               ["ou"] + xkeys, ["sta%d" % h])
+            quant(sk, HF * h, HF, T.st, ["sta%d" % h, "stb%d" % h], ["q%sh%d" % (sk, h)])
+            if h == cross:
+                for kind in (0, 1):
+                    xs = []
+                    for i, hc in enumerate(helpers[rank][kind]):
+                        a = HF * h + 2 * PC * i
+                        xs.append(_xfer(topo, core, [(hc, _view(T, kind, rk, 0, 2 * PC))], _view(T, kind, sk, a, a + 2 * PC),
+                                        on[i::2], T.sem["hr%d" % t]))
+                    send(xs, len(on), ["q%sh%d" % (sk, h)])
+            else:
+                q4 = len(off) // 4
+                share = ((off[:2 * q4], off[2 * q4:3 * q4], off[3 * q4:]), (off[2 * q4:], off[:q4], off[q4:2 * q4]))
+                for kind in (0, 1):
+                    xs = [_xfer(topo, core, [(cores[order[j]], _view(T, kind, lk, _slot(me, j), _slot(me, j) + PC))],
+                                _view(T, kind, sk, j * PC, j * PC + PC), share[kind][n], T.sem["ra%d" % t])
+                          for n, j in enumerate(peers)]
+                    send(xs, len(off), ["q%sh%d" % (sk, h)])
+                op("V", lambda: V.tensor_copy(T["q" + lk][:, 0:128].bitcast(dt.uint32),
+                                              T["q" + sk][:, HF * h:HF * h + HF].bitcast(dt.uint32).indirect(T.oo[:, 0:8])),
+                   ["q%sh%d" % (sk, h), "oo"], [lk + "q"])
+                op("S", lambda: S.activation(T["s" + lk][:, 0:128], T["s" + sk][:, HF * h:HF * h + HF].indirect(T.oo[:, 0:8]), F.Copy),
+                   ["q%sh%d" % (sk, h), "oo"], [lk + "s"])
+        arrives(lk + "h%d" % mine, "ra%d" % t, 2 * len(off))
+        arrives(lk + "h%d" % cross, "rb%d" % t, 4 * len(off))
+
+        if t == 0:
+            fk = ["ft%d" % b for b in range(4)]
+            op("S", lambda: S.activation(T.et[:], T.ft[:], F.Copy, scale=8.0), fk, ["et"])
+            quant("f", 0, 512, T.ft, fk, ["qf"])
+            op("V", lambda: V.memset(T.mt[:], 0.0), [], ["mt0", "mt1", "mt2", "mt3"])
+            op("V", lambda: V.memset(T.ht[:], 0.0), [], ["ht0", "ht1", "ht2", "ht3"])
+            quant("v", 0, 128, T.vt, ["vt"], ["qv"])
+            quant("e", 0, 512, T.et, ["et"], ["qe"])
+        if t == R - 1:
+            ts(T.olf[:], T.ob[:], 1.0 * HF, None, A.add, None, ["ob"], ["olf"])
+            dma("Y", "dout", [(T.ol[k:k + 1, :], T.olf[16 * k:16 * k + 1, :]) for k in range(8)],
+                ["olf", lk + "h%d" % mine], [])
+
+        for h in (mine, cross):
+            for b in range(3):
+                mm((2 if h == mine else 5) + b, T.qf, T.sf, 128 * b, lk, PAD + (0 if h == mine else HF), HF,
+                   ["qf", lk + "h%d" % h, lk + "q", lk + "s"])
+        for r in range(N):
+            mm(0, T.qf, T.sf, 128 * 3, lk, _slot(order.index(r), me) - PAD, 128, ["qf", lk + "h0", lk + "h1"], r == 0, r == N - 1)
+        seq = list(range(N))
+        if order.index(0) // 4 != mine and order.index(1) // 4 == mine:
+            seq[0], seq[1] = 1, 0
+        for n, r in enumerate(seq):
+            k = order.index(r)
+            for b in range(3):
+                bk = (2 if k // 4 == mine else 5) + b
+                a = (_slot(k, me) - PAD) % HF
+                src, acc = bank(bk, a, a + PC), T.acc[:, b * PC:b * PC + PC]
+                if n == 0:
+                    op("V", lambda: V.tensor_copy(acc, src), ["B%d" % bk], ["acc%d" % b])
+                elif n < N - 1:
+                    op("V", lambda: V.tensor_tensor(acc, src, acc, A.add), ["B%d" % bk], ["acc%d" % b])
+                else:
+                    op("V", lambda: V.tensor_tensor(T.mt[:, 4 * PAD + b:512:4], src, acc, A.add), ["B%d" % bk, "acc%d" % b], ["mt%d" % b])
+        op("S", lambda: S.activation(T.mt[:, 4 * PAD + 3:512:4], bank(0, PAD, 128), F.Copy), ["B0"], ["mt3"])
+        quant("m", 0, 128, T.mt, ["mt0", "mt1", "mt2", "mt3"], ["qm"])
+        for b in range(4):
+            mm(b, T.qw, T.sw, 128 * b, "m", 0, 128, ["qw", "qm"])
+        for b in range(4):
+            if b % 2 == 0:
+                op("S", lambda: S.activation(T.ht[:, 4 * PAD + b:512:4], bank(b, PAD, 128), F.Relu, scale=0.0625), ["B%d" % b], ["ht%d" % b])
+            else:
+                ts(T.ht[:, 4 * PAD + b:512:4], bank(b, PAD, 128), 0.0, 0.0625, A.max, A.mult, ["B%d" % b], ["ht%d" % b])
+        quant(gk, 0, 128, T.ht, ["ht0", "ht1", "ht2", "ht3"], [gk + "q"])
+
+        for kind in (0, 1):
+            src = _view(T, kind, gk, PAD, 128)
+            send([_xfer(topo, core, [(hc, _view(T, kind, ak, 0, PC)) for hc in helpers[rank][kind]], src, rest, T.sem["ha%d" % t]),
+                  _xfer(topo, core, [(cores[order[j]], _view(T, kind, gk, _slot(me, j), _slot(me, j) + PC)) for j in peers], src, off,
+                        T.sem["ga%d" % t])], len(on), [gk + "q"])
+        arrives(gk + "h%d" % mine, "ga%d" % t, 6 * len(off))
+        arrives(gk + "h%d" % cross, "gb%d" % t, 4 * len(off))
+
+        for n, h in enumerate((mine, cross)):
+            for b in range(4):
+                mm(4 * n + b, T.qe, T.se, 128 * b, gk, PAD + HF * n, HF, ["qe", gk + "q", gk + "h%d" % h])
+        for n, h in enumerate((mine, cross)):
+            turn = PC * (me % 4) if n == 0 else 0
+            for b in range(4):
+                for m, (a, z, p0) in enumerate(((0, HF - turn, HF * h + turn), (HF - turn, HF, HF * h))):
+                    if z > a:
+                        op("V", lambda: V.tensor_tensor(T.sn[:, C * b + p0:C * b + p0 + z - a], bank(4 * n + b, a, z),
+                                                        T.st[:, 4 * p0 + b:4 * (p0 + z - a):4], A.add),
+                           ["B%d" % (4 * n + b), "sta%d" % h, "stb%d" % h], ["sn%d%d%d" % (b, h, m)])
+        XN = T[xn]
+
+        def back(q, b, h):
+            out = XN[:, 4 * HF * h + b:4 * HF * (h + 1):4]
+            win = T.sn[:, C * b:C * b + C].indirect(T.iu[:, (NS // 2) * h:(NS // 2) * (h + 1)])
+            reads = ["sn%d%d%d" % (b, h2, m) for h2 in range(2) for m in range(2)] + ["iu0", "iu1", "iu2"]
+            if q == "S":
+                op("S", lambda: S.activation(out, win, F.Copy, scale=0.5), reads, [xn + "_%d%d" % (b, h)])
+            else:
+                ts(out, win, 0.5, None, A.mult, None, reads, [xn + "_%d%d" % (b, h)])
+
+        for b, h in ((0, 0), (1, 0), (0, 1), (1, 1), (2, 1)):
+            back("S", b, h)
+        back("V", 2, 0)
+        back("V", 3, 0)
+        quant(xn, 0, HF, XN, [xn + "_%d0" % b for b in range(4)], ["q" + xn + "h0"])
+        back("V", 3, 1)
+        quant(xn, HF, HF, XN, [xn + "_%d1" % b for b in range(4)], ["q" + xn + "h1"])
+
+    xk = "x%d" % R
+    for h in range(2):
+        a, z = HF * h, HF * h + HF
+        mm(h, T.qv, T.sv, 0, xk, a, HF, ["qv", "q%sh%d" % (xk, h)])
+        dma("Y", "dout", [(T.oc[:, 4 * a:4 * z], _view(T, 0, xk, a, z))], ["q%sh%d" % (xk, h)], [])
+        if h == 0:
+            op("S", lambda: S.activation(T.yt[:, a:z], bank(h, 0, HF), F.Copy), ["B%d" % h], ["yt%d" % h])
+        else:
+            op("V", lambda: V.tensor_copy(T.yt[:, a:z], bank(h, 0, HF)), ["B%d" % h], ["yt%d" % h])
+        dma("S", "dout", [(T.y[:, a:z], T.yt[:, a:z])], ["yt%d" % h], [])
+    dma("Y", "dout", [(T.osc[4 * k:4 * k + 4, :], T["s" + xk][32 * k:32 * k + 4, :]) for k in range(4)],
+        ["q%sh0" % xk, "q%sh1" % xk], [])
+    for sem, n in total.items():
+        if waited.get(sem, 0) < n:
+            g.wait_ge(T.sem[sem], n)

@@ -5,9 +5,17 @@ C, R, N = 448, 2, 8
 PC = C // N
 HF = C // 2
 NS = C // 16
-HI, LO = 6, 20
+SL = NS // 2
+RW = 8 * SL
+LAG = 2
+CUTS = (0, 8, 14, 22, 28)
+SUBS = ((0, 112), (112, 224), (224, 336), (336, 448))
+BIG, LEAD = 2.0 ** 90, 32.0
+HEAD = "m3 m2 f3 m1 f2 m0 f1 f0"
+PLAN = ("ud e uc n ub ua u9 u8 u7 u6 u5 u4 u3 u2 u1 u0 s0 s1 s2 s3 c1 c0 d1 s4 d0 s5 s6 t00 t01 s7 s8 c2 g00 g01 s9 sa c3 d2 sb d3 "
+        "sc sd r1 t10 t11 r0 g10 r2 g11 p0 p1 p2 p3")
+SPLAN = [("w", s) for s in range(NS - 1, SL, -1)] + [("u", s) for s in range(SL, NS - 1)]
 PAD = 128 - PC
-SW = 464
 X4, U8, BF, F32 = "float8_e4m3fn_x4", "uint8", "bfloat16", "float32"
 
 SCRATCH = {
@@ -20,15 +28,17 @@ SCRATCH = {
     "eighth": ("sbuf", [128, 512], BF), "ft": ("sbuf", [128, 2048], BF), "et": ("sbuf", [128, 2048], BF),
     "qf": ("sbuf", [128, 512], X4), "sf": ("sbuf", [128, 512], U8),
     "qe": ("sbuf", [128, 512], X4), "se": ("sbuf", [128, 512], U8),
-    "pi": ("sbuf", [128, 8], "int32"), "pf": ("sbuf", [128, 12], F32),
+    "pi": ("sbuf", [128, 8], "int32"), "pf": ("sbuf", [128, 16], F32),
     "ui": ("sbuf", [128, 8], "int32"), "uo": ("sbuf", [128, 8], "uint16"), "oo": ("sbuf", [128, 8], "uint16"),
-    "t16": ("sbuf", [128, C], BF), "jv": ("sbuf", [128, C], BF),
-    "hot": ("sbuf", [128, C], BF), "keep": ("sbuf", [128, C], BF),
-    "k4": ("sbuf", [128, 12], F32), "k2": ("sbuf", [128, C], BF),
-    "msk": ("sbuf", [128, C], F32), "fill": ("sbuf", [128, C], F32),
-    "eq": ("sbuf", [128, C], BF), "nc": ("sbuf", [128, C], BF),
-    "fl": ("sbuf", [128, 4 * C], BF), "so": ("sbuf", [128, (LO - HI) * HF], "float16"),
-    "sg": ("sbuf", [128, (HI + NS - LO) * SW], BF), "ac": ("sbuf", [128, 16], F32),
+    "t16": ("sbuf", [128, C], BF), "t32": ("sbuf", [128, 32], BF), "jv": ("sbuf", [128, C], BF),
+    "jump": ("sbuf", [128, C], BF), "cap": ("sbuf", [128, C], BF), "keep": ("sbuf", [128, C], BF),
+    "own": ("sbuf", [128, 256], BF), "k4": ("sbuf", [128, 12], F32), "k2": ("sbuf", [128, C], BF),
+    "msk": ("sbuf", [128, C], F32), "fill": ("sbuf", [128, C], F32), "nc": ("sbuf", [128, C], BF),
+    "f0": ("sbuf", [128, 8 * C], BF), "f1": ("sbuf", [128, 8 * C], BF), "so": ("sbuf", [128, SL * RW], "float16"),
+    "sg": ("sbuf", [128, 8 * C], BF), "ac": ("sbuf", [128, 2 * NS], F32),
+    "pb": ("sbuf", [128, 8 * (C + len(SUBS))], "float16"), "cs": ("sbuf", [128, C + 32], BF),
+    "tu": ("sbuf", [128, 2 * C + 32], BF), "us": ("sbuf", [128, 2 * C + 32], BF),
+    "rr": ("sbuf", [128, NS], F32), "r0": ("sbuf", [128, NS], F32), "r1": ("sbuf", [128, NS], F32), "r2": ("sbuf", [128, NS], F32),
     "iu": ("sbuf", [128, NS], "uint16"), "ob": ("sbuf", [128, C], BF), "ox": ("sbuf", [128, C], "float16"),
     "ou": ("sbuf", [128, C // 4], "uint16"), "olf": ("sbuf", [128, C], F32),
     "st": ("sbuf", [128, 4 * C], BF), "acc": ("sbuf", [128, 3 * PC], F32),
@@ -187,6 +197,12 @@ def rank_program(g, core, T, topo):
         else:
             op("V", lambda: V.tensor_scalar(out, in0, s1, s2, o0, o1), reads, writes)
 
+    def tt(out, in0, in1, o, reads, writes):
+        op("V", lambda: V.tensor_tensor(out, in0, in1, o), reads, writes)
+
+    def scan(out, d0, d1, first, o0, o1, reads, writes):
+        op("V", lambda: V.tensor_tensor_scan(out, d0, d1, first, o0, o1), reads, writes)
+
     me = order.index(rank)
     mine, cross = me // 4, 1 - me // 4
     peers = [4 * mine + (me + d) % 4 for d in (1, 2, 3)]
@@ -194,108 +210,183 @@ def rank_program(g, core, T, topo):
     off = topo.engines(core, cores[order[peers[0]]])
     rest = [e for e in on if e not in off]
 
+    def flags(s, a, z):
+        k = SL if s == NS else s % SL
+        return T["f%d" % (k // 8)][:, 8 * a + k % 8:8 * z:8]
+
     dma("S", "du", [(T.ut[:], T.u[:])], [], ["ut"])
     dma("Y", "dxa", [(T.x0[:, 0:4 * HF], T.x[:, 0:4 * HF])], [], ["x0h0"])
     dma("Y", "dxb", [(T.x0[:, 4 * HF:4 * C], T.x[:, 4 * HF:4 * C])], [], ["x0h1"])
-    op("G", lambda: g.iota(T.pi[:, 0:1], [[0, 1]], 0, 1), [], ["pi0"])
-    op("G", lambda: g.iota(T.ui[:], [[16, 8]], 0, 0), [], ["ui"])
     small = dict(allow_small_or_imprecise_dtypes=True)
+    op("G", lambda: g.iota(T.pi[:, 0:1], [[0, 1]], 0, 1), [], ["pi0"])
+    op("G", lambda: g.iota(T.t32[:], [[1, 32]], 0, 0, **small), [], ["t32"])
+    op("G", lambda: g.iota(T.ui[:], [[16, 8]], 0, 0), [], ["ui"])
     op("G", lambda: g.iota(T.t16[:], [[0, NS], [1, 16]], 0, 0, **small), [], ["t16"])
+    op("G", lambda: g.iota(T.f1[:, 7:8 * C:8], [[0, C]], 0, 0, **small), [], ["z"])
+    for s in range(SL):
+        op("G", lambda: g.iota(flags(s, 16 * s, 16 * s + 16), [[0, 16]], 0, 0, **small), [], ["z%d" % s])
     op("G", lambda: g.iota(T.jv[:], [[1, C]], -HF, 0, **small), [], ["jv"])
     op("V", lambda: V.memset(T.eighth[:], 0.125), [], ["eighth"])
-    op("V", lambda: V.memset(T.ob[:], 0.0), [], ["ob"])
+    ts(T.pi[:, 4:5], T.pi[:, 0:1], 4, 1, A.logical_shift_right, A.bitwise_and, ["pi0"], ["pi4"])
     ts(T.pi[:, 1:2], T.pi[:, 0:1], 15, None, A.bitwise_and, None, ["pi0"], ["pi1"])
     ts(T.pi[:, 2:3], T.pi[:, 0:1], 2, 3, A.logical_shift_right, A.bitwise_and, ["pi0"], ["pi2"])
     ts(T.pi[:, 3:4], T.pi[:, 0:1], 3, None, A.bitwise_and, None, ["pi0"], ["pi3"])
+    op("V", lambda: V.memset(T.ac[:], 0.0), [], ["au%d" % s for s in range(NS)] + ["aw%d" % s for s in range(NS)])
+    op("V", lambda: V.tensor_copy(T.pf[:, 0:5], T.pi[:, 0:5]), ["pi0", "pi1", "pi2", "pi3", "pi4"], ["pf"])
     op("V", lambda: V.tensor_copy(T.uo[:], T.ui[:]), ["ui"], ["uo"])
-    op("V", lambda: V.tensor_copy(T.pf[:, 0:4], T.pi[:, 0:4]), ["pi0", "pi1", "pi2", "pi3"], ["pf"])
-    ts(T.pf[:, 4:5], T.pf[:, 2:3], 0.0, 4.0, A.is_equal, A.mult, ["pf"], ["pf4"])
+    ts(T.pf[:, 10:11], T.pf[:, 4:5], 512.0, -256.0, A.mult, A.add, ["pf"], ["pf10"])
+    ts(T.pf[:, 11:12], T.pf[:, 4:5], -512.0 * 15.5, 256.0 * 15.5, A.mult, A.add, ["pf"], ["pf11"])
+    op("S", lambda: S.activation(T.own[:, 0:32], T.t32[:], F.Sigmoid, bias=T.pf[:, 11:12], scale=T.pf[:, 10:11]),
+       ["t32", "pf10", "pf11"], ["own"])
+    ts(T.pf[:, 5:6], T.pf[:, 2:3], 0.0, 4.0, A.is_equal, A.mult, ["pf"], ["pf5"])
     ts(T.pf[:, 8:9], T.pf[:, 1:2], float(PC * (me % 4) - PAD), None, A.add, None, ["pf"], ["pf8"])
-    ts(T.pf[:, 5:6], T.pf[:, 4:5], T.pf[:, 2:3], -1.0, A.add, A.add, ["pf", "pf4"], ["pf5"])
-    ts(T.pf[:, 6:7], T.pf[:, 4:5], 2.0 * C, T.pf[:, 3:4], A.mult, A.add, ["pf", "pf4"], ["pf6"])
-    ts(T.oo[:], T.ui[:], T.pf[:, 8:9], 0.0, A.add, A.max, ["ui", "pf8"], ["oo"])
-    ts(T.pf[:, 7:8], T.pf[:, 6:7], -4.0 * HF, None, A.add, None, ["pf6"], ["pf7"])
-    ts(T.k4[:, 0:4], T.t16[:, 0:4], T.pf[:, 2:3], 1.0 * C, A.is_equal, A.mult, ["pf", "t16"], ["ka"])
-    ts(T.k4[:, 4:8], T.t16[:, 0:4], T.pf[:, 5:6], -2.0 * C, A.is_equal, A.mult, ["pf5", "t16"], ["kb"])
-    ts(T.hot[:], T.t16[:], T.pf[:, 1:2], None, A.is_equal, None, ["pf", "t16"], ["hot"])
-    op("V", lambda: V.tensor_tensor(T.k4[:, 8:12], T.k4[:, 0:4], T.k4[:, 4:8], A.add), ["ka", "kb"], ["k4"])
-    ts(T.keep[:], T.t16[:], T.pf[:, 1:2], None, A.not_equal, None, ["pf", "t16"], ["keep"])
+    ts(T.pf[:, 9:10], T.pf[:, 1:2], 0.25, None, A.add, None, ["pf"], ["pf9"])
+    ts(T.pf[:, 12:13], T.pf[:, 5:6], T.pf[:, 2:3], -1.0, A.add, A.add, ["pf", "pf5"], ["pf12"])
+    ts(T.pf[:, 6:7], T.pf[:, 5:6], 2.0 * C, T.pf[:, 3:4], A.mult, A.add, ["pf", "pf5"], ["pf6"])
+    ts(T.k4[:, 0:4], T.t32[:, 0:4], T.pf[:, 2:3], 1.0 * C, A.is_equal, A.mult, ["pf", "t32"], ["ka"])
+    ts(T.k4[:, 4:8], T.t32[:, 0:4], T.pf[:, 12:13], -2.0 * C, A.is_equal, A.mult, ["pf12", "t32"], ["kb"])
+    op("V", lambda: V.memset(T.cs[:], 0.0), [], ["cs%d" % n for n in range(len(SUBS))])
+    op("V", lambda: V.memset(T.ob[:], 0.0), [], ["ob"])
+    ts(T.jump[:], T.t16[:], T.pf[:, 1:2], 2 * BIG, A.is_equal, A.mult, ["pf", "t16"], ["jump"])
+    tt(T.k4[:, 8:12], T.k4[:, 0:4], T.k4[:, 4:8], A.add, ["ka", "kb"], ["k4"])
+    ts(T.keep[:], T.t16[:], 0.0, None, A.not_equal, None, ["t16"], ["keep"])
     quant("u", 0, 128, T.ut, ["ut"], ["qu"])
-    for b in range(2):
-        ts(T.k2[:, b:C:4], T.t16[:, 0:C // 4], 0.0, T.k4[:, 8 + b:9 + b], A.mult, A.add, ["k4", "t16"], ["k2%d" % b])
+    ts(T.cap[:], T.jump[:], -1.0, BIG, A.mult, A.add, ["jump"], ["cap"])
     op("V", lambda: V.tensor_copy(T.qp[:].bitcast(dt.uint32), T.qu[:].bitcast(dt.uint32).indirect(T.uo[:, 0:8])),
        ["qu", "uo"], ["qp"])
     op("S", lambda: S.activation(T.sp[:], T.su[:].indirect(T.uo[:, 0:8]), F.Copy), ["qu", "uo"], ["sp"])
-    for b in range(2, 4):
-        ts(T.k2[:, b:C:4], T.t16[:, 0:C // 4], 0.0, T.k4[:, 8 + b:9 + b], A.mult, A.add, ["k4", "t16"], ["k2%d" % b])
+    ts(T.jump[:, 0:C:16], T.t16[:, 0:NS], 0.0, 2 * BIG, A.mult, A.add, ["t16"], ["jump"])
+    quant("x0", 0, HF, T.x0, ["x0h0"], ["qx0h0"])
+    quant("x0", HF, HF, T.x0, ["x0h1"], ["qx0h1"])
+    ts(T.pf[:, 7:8], T.pf[:, 6:7], -4.0 * HF, None, A.add, None, ["pf6"], ["pf7"])
+    ts(T.oo[:], T.ui[:], T.pf[:, 8:9], 0.0, A.add, A.max, ["ui", "pf8"], ["oo"])
+    for n, (a, z) in enumerate(SUBS):
+        ts(T.pb[:, 8 * (a + n):8 * (a + n + 1)], T.t32[:, 0:8], 0.0, LEAD, A.mult, A.add, ["t32"], ["lead%d" % n])
+    for b in range(4):
+        if b < 3:
+            n = 32 << b
+            op("S", lambda: S.activation(T.own[:, n:2 * n], T.own[:, 0:n], F.Copy), ["own"], ["own"])
+        op("S", lambda: S.activation(T.k2[:, b:C:4], T.t16[:, 0:C // 4], F.Identity, bias=T.k4[:, 8 + b:9 + b], scale=0.0),
+           ["k4", "t16"], ["k2%d" % b])
     for b in range(4):
         op("G", lambda: g.affine_select(T.ft[:, 512 * b:512 * b + 512], T.eighth[:], [[-1, 512]], A.is_equal, 0.0, b, 4),
            ["eighth"], ["ft%d" % b])
-    for h in range(2):
-        quant("x0", HF * h, HF, T.x0, ["x0h%d" % h], ["qx0h%d" % h])
     dma("Y", "dw", [(T.qw[:].bitcast(dt.uint8), T.wc[:]), (T.sw[:], T.ws[:])], ["x0h1"], ["qw"])
     dma("Y", "dv", [(T.vt[:], T.v[:])], [], ["vt"])
+
+    up = {s: (16 * s + 16, min(C, 16 * (s + 1 + (SL if s < SL else SL - 1)))) for s in range(NS - 1)}
+    wrap = {s: (0, 16 * (s - SL)) for s in range(SL + 1, NS)}
 
     for t in range(R):
         xk, xn = "x%d" % t, "x%d" % (t + 1)
         xkeys = [xk + "h0", xk + "h1"] if t == 0 else [xk + "_%d%d" % (b, h) for b in range(4) for h in range(2)]
         for b in range(2):
             mm(b, T.qp, T.sp, 0, xk, 0, C, ["qp", "sp", "q" + xk + "h0", "q" + xk + "h1"])
-        cuts = ((0, 128), (128, C))
-        for n, (a, z) in enumerate(cuts):
-            op("V", lambda: V.tensor_tensor(T.msk[:, a:z], bank(0, a, z), T.hot[:, a:z], A.mult), ["B0", "hot"], ["msk%d" % n])
-            op("V", lambda: V.tensor_tensor_scan(T.fill[:, a:z], T.keep[:, a:z], T.msk[:, a:z], 0.0, A.mult, A.add),
-               ["keep", "msk%d" % n], ["fill%d" % n])
+
+        def msk(n):
+            a, z = 16 * CUTS[n], 16 * CUTS[n + 1]
+            tt(T.msk[:, a:z], bank(0, a, z), T.cap[:, a:z], A.max, ["B0", "cap"], ["msk%d" % n])
+
+        def fill(n):
+            a, z = 16 * CUTS[n], 16 * CUTS[n + 1]
+            scan(T.fill[:, a:z], T.jump[:, a:z], T.msk[:, a:z], 0.0, A.add, A.min, ["jump", "msk%d" % n], ["fill%d" % n])
 
         def zc(s):
             return T.fill[:, 16 * s + 15:16 * s + 16]
 
         def zk(s):
-            return "fill0" if s < 8 else "fill1"
+            return "fill%d" % max(n for n in range(len(CUTS) - 1) if CUTS[n] <= s)
 
-        outer = list(range(HI)) + list(range(LO, NS))
-        for n, s in enumerate(outer):
-            a, z = (16 * s + 16, C) if s < HI else (0, 16 * s + 16)
-            op("S", lambda: S.activation(T.sg[:, n * SW + a:n * SW + z], bank(1, a, z), F.Sign, bias=zc(s), scale=-1.0),
-               ["B1", zk(s)], ["sga%d" % n])
-        op("V", lambda: V.tensor_tensor(T.eq[:], bank(0, 0, C), T.fill[:], A.is_equal), ["B0", "fill0", "fill1"], ["eq"])
-        for n, s in enumerate(outer):
-            if s < HI:
-                ts(T.sg[:, n * SW:n * SW + 16 * s + 16], bank(0, 0, 16 * s + 16), zc(s), -1.0, A.is_ge, A.mult,
-                   ["B0", zk(s)], ["sgb%d" % n])
-            if n == 0:
-                op("V", lambda: V.tensor_tensor_scan(T.nc[:], T.keep[:], T.eq[:], 0.0, A.mult, A.subtract), ["keep", "eq"], ["nc"])
-            if LO <= s < NS - 1:
-                ts(T.sg[:, n * SW + 16 * s + 16:n * SW + C], bank(0, 16 * s + 16, C), zc(s), None, A.is_le, None,
-                   ["B0", zk(s)], ["sgb%d" % n])
-        ts(T.sg[:, C:HI * SW:SW], T.nc[:, 15:16 * HI:16], -1.0, -16.0, A.mult, A.add, ["nc"], ["sgc0"])
-        ts(T.sg[:, HI * SW + C:len(outer) * SW:SW], T.nc[:, 16 * LO + 15:C:16], -1.0, None, A.mult, None, ["nc"], ["sgc1"])
-        for n, s in enumerate(outer):
-            row = T.sg[:, n * SW:n * SW + C + 1]
-            c = "sgc0" if s < HI else "sgc1"
-            op("S", lambda: S.activation(row, row, F.Relu, scale=-1.0 if s < HI else 1.0, accum_out=T.ac[:, n:n + 1]),
-               [c], ["sga%d" % n, "sgb%d" % n, "ac%d" % n])
+        for w in HEAD.split():
+            (msk if w[0] == "m" else fill)(int(w[1]))
+        at = [0]
 
-        def scan(s):
-            f = (s % 4) * C
-            op("V", lambda: V.tensor_tensor_scan(T.so[:, (s - HI) * HF:(s - HI + 1) * HF], T.fl[:, f:f + HF], T.fl[:, f + HF:f + C],
-                                                 T.nc[:, 16 * s + 15:16 * s + 16], A.add, A.add),
-               ["fa%d" % (s % 4), "fb%d" % (s % 4), "nc"], ["so%d" % s])
+        def sign(n):
+            k, s = SPLAN[n]
+            a, z = (up if k == "u" else wrap)[s]
+            at.append(at[-1] + z - a)
+            op("S", lambda: S.activation(T.sg[:, at[n]:at[n + 1]], bank(1, a, z), F.Sign, bias=zc(s), scale=-1.0),
+               ["B1", zk(s)], ["sg%d" % n])
 
-        for s in range(HI, LO):
-            f, m = (s % 4) * C, 16 * s + 16
-            ts(T.fl[:, f:f + m], bank(0, 0, m), zc(s), None, A.is_ge, None, ["B0", zk(s)], ["fa%d" % (s % 4)])
-            ts(T.fl[:, f + m:f + C], bank(0, m, C), zc(s), None, A.is_gt, None, ["B0", zk(s)], ["fb%d" % (s % 4)])
-            if s > HI:
-                scan(s - 1)
-        ts(T.iu[:, 0:HI], T.ac[:, 0:HI], -16.0, None, A.add, None, ["ac%d" % n for n in range(HI)], ["iu0"])
-        scan(LO - 1)
-        op("V", lambda: V.tensor_copy(T.iu[:, HI:LO], T.so[:, HF - 1:(LO - HI) * HF:HF]), ["so%d" % s for s in range(HI, LO)], ["iu1"])
-        op("V", lambda: V.tensor_copy(T.ob[:, 0:C].indirect(T.iu[:, 0:LO]), T.jv[:, 0:16 * LO]), ["iu0", "iu1", "jv"], ["ob"])
-        ts(T.iu[:, LO:NS], T.ac[:, HI:len(outer)], -1.0, 1.0 * C, A.mult, A.add, ["ac%d" % n for n in range(HI, len(outer))], ["iu2"])
-        op("V", lambda: V.tensor_copy(T.ob[:, 0:C].indirect(T.iu[:, LO:NS]), T.jv[:, 16 * LO:C]), ["iu2", "jv"], ["ob"])
-        op("V", lambda: V.tensor_tensor_scan(T.ox[:], T.ob[:], T.k2[:], -1000.0, A.max, A.add),
-           ["ob", "k20", "k21", "k22", "k23"], ["ox"])
+        def flag(n):
+            k, s = SPLAN[n]
+            a, z = (up if k == "u" else wrap)[s]
+            src = T.sg[:, at[n]:at[n + 1]]
+            if k == "u":
+                op("S", lambda: S.activation(flags(s, a, z), src, F.Relu, scale=-1.0, accum_out=T.ac[:, s:s + 1]),
+                   ["sg%d" % n], ["Fu%d" % s, "au%d" % s])
+            else:
+                op("S", lambda: S.activation(flags(s, a, z), src, F.Sigmoid, bias=128.0, scale=-256.0,
+                                             accum_out=T.ac[:, NS + s:NS + s + 1]), ["sg%d" % n], ["Fw%d" % s, "aw%d" % s])
+
+        for n in range(len(SPLAN) + LAG):
+            if n < len(SPLAN):
+                sign(n)
+            if n >= LAG:
+                flag(n - LAG)
+
+        def row(s):
+            a, z = up[s]
+            ts(flags(s, a, z), bank(0, a, z), zc(s), None, A.is_gt, None, ["B0", zk(s)], ["Fu%d" % s])
+
+        def inside():
+            tt(flags(NS, 0, C), bank(0, 0, C), T.fill[:], A.is_gt, ["B0"] + ["fill%d" % n for n in range(len(CUTS) - 1)], ["D"])
+
+        def inrow():
+            scan(T.nc[:], T.keep[:], flags(NS, 0, C), 0.0, A.mult, A.add, ["keep", "D"], ["nc"])
+
+        def rsum(s):
+            a, z = up[s]
+            m = (a + z) // 2
+            scan(T.so[:, s * RW:(s + 1) * RW], flags(s, a, m), flags(s, m, z), T.nc[:, 16 * s + 15:16 * s + 16], A.add, A.add,
+                 ["Fu%d" % s, "nc"], ["so%d" % s])
+
+        def col(n):
+            a, z = SUBS[n]
+            keys = ["Fu%d" % s for s in up if up[s][0] < z and up[s][1] > a] + ["Fw%d" % s for s in wrap if wrap[s][1] > a]
+            scan(T.pb[:, 8 * (a + n + 1):8 * (z + n + 1)], T.f0[:, 8 * a:8 * z], T.f1[:, 8 * a:8 * z], LEAD, A.add, A.add,
+                 keys + ["D", "z"] + ["z%d" % s for s in range(SL)], ["pb%d" % n])
+
+        def diff(n):
+            a, z = SUBS[n]
+            scan(T.cs[:, 16 + a:16 + z], T.pb[:, 8 * (a + n + 1) + 7:8 * (z + n + 1):8], T.pb[:, 8 * (a + n) + 7:8 * (z + n):8],
+                 0.0, A.max, A.subtract, ["pb%d" % n, "lead%d" % n], ["cs%d" % n])
+
+        def piece(c, w):
+            return (16 + HF * c, HF, HF * c) if w == 0 else (HF * c, HF + 32 * c, C + HF * c)
+
+        def turn(c, w):
+            a, n, o0 = piece(c, w)
+            keys = ["cs%d" % k for k in range(len(SUBS)) if SUBS[k][0] + 16 < a + n and SUBS[k][1] + 16 > a]
+            op("V", lambda: V.transpose(T.tu[:, o0:o0 + n], T.cs[:, a:a + n]), keys, ["tu%d%d" % (c, w)])
+
+        def gsum(c, w):
+            a, n, o0 = piece(c, w)
+            scan(T.us[:, o0:o0 + n], T.tu[:, o0:o0 + n], T.own[:, 0:n], 0.0, A.add, A.mult, ["tu%d%d" % (c, w), "own"], ["us%d%d" % (c, w)])
+
+        def rows(w):
+            if w == 0:
+                ts(T.rr[:, 0:SL], T.so[:, RW - 1:SL * RW:RW], -16.0, None, A.add, None, ["so%d" % s for s in range(SL)], ["rr0"])
+            elif w == 1:
+                tt(T.r0[:, SL:NS], T.ac[:, NS + SL:2 * NS], T.nc[:, HF + 15:C:16], A.add,
+                   ["nc"] + ["aw%d" % s for s in range(SL, NS)], ["rs"])
+            else:
+                tt(T.rr[:, SL:NS], T.r0[:, SL:NS], T.ac[:, SL:NS], A.add, ["rs"] + ["au%d" % s for s in range(SL, NS)], ["rr1"])
+
+        def place(w):
+            if w == 0:
+                tt(T.r1[:], T.rr[:], T.us[:, 15:C:16], A.subtract, ["rr0", "rr1", "us00", "us10"], ["r1"])
+            elif w == 1:
+                tt(T.r2[:], T.r1[:], T.us[:, C + 31:2 * C + 16:16], A.subtract, ["r1", "us01", "us11"], ["r2"])
+            elif w == 2:
+                ts(T.iu[:], T.r2[:], T.pf[:, 9:10], 16.0 * SL, A.add, A.add, ["r2", "pf9"], ["iu"])
+            else:
+                op("V", lambda: V.tensor_copy(T.ob[:, 0:C].indirect(T.iu[:, 0:NS]), T.jv[:]), ["iu", "jv"], ["ob"])
+
+        calls = {"u": row, "e": inside, "n": inrow, "c": col, "d": diff, "t": turn, "g": gsum, "r": rows, "p": place, "s": rsum}
+        for w in PLAN.split():
+            calls[w[0]](*[int(ch, 16) for ch in w[1:]])
+        scan(T.ox[:], T.ob[:], T.k2[:], -1000.0, A.max, A.add, ["ob", "k20", "k21", "k22", "k23"], ["ox"])
         ts(T.ou[:], T.ox[:, 3:C:4], 4.0, T.pf[:, 7:8], A.mult, A.add, ["ox", "pf7"], ["ou"])
 
         X = T[xk]
@@ -362,9 +453,9 @@ def rank_program(g, core, T, topo):
                 if n == 0:
                     op("V", lambda: V.tensor_copy(acc, src), ["B%d" % bk], ["acc%d" % b])
                 elif n < N - 1:
-                    op("V", lambda: V.tensor_tensor(acc, src, acc, A.add), ["B%d" % bk], ["acc%d" % b])
+                    tt(acc, src, acc, A.add, ["B%d" % bk], ["acc%d" % b])
                 else:
-                    op("V", lambda: V.tensor_tensor(T.mt[:, 4 * PAD + b:512:4], src, acc, A.add), ["B%d" % bk, "acc%d" % b], ["mt%d" % b])
+                    tt(T.mt[:, 4 * PAD + b:512:4], src, acc, A.add, ["B%d" % bk, "acc%d" % b], ["mt%d" % b])
         op("S", lambda: S.activation(T.mt[:, 4 * PAD + 3:512:4], bank(0, PAD, 128), F.Copy), ["B0"], ["mt3"])
         quant("m", 0, 128, T.mt, ["mt0", "mt1", "mt2", "mt3"], ["qm"])
         for b in range(4):
@@ -388,19 +479,18 @@ def rank_program(g, core, T, topo):
             for b in range(4):
                 mm(4 * n + b, T.qe, T.se, 128 * b, gk, PAD + HF * n, HF, ["qe", gk + "q", gk + "h%d" % h])
         for n, h in enumerate((mine, cross)):
-            turn = PC * (me % 4) if n == 0 else 0
+            rot = PC * (me % 4) if n == 0 else 0
             for b in range(4):
-                for m, (a, z, p0) in enumerate(((0, HF - turn, HF * h + turn), (HF - turn, HF, HF * h))):
+                for m, (a, z, p0) in enumerate(((0, HF - rot, HF * h + rot), (HF - rot, HF, HF * h))):
                     if z > a:
-                        op("V", lambda: V.tensor_tensor(T.sn[:, C * b + p0:C * b + p0 + z - a], bank(4 * n + b, a, z),
-                                                        T.st[:, 4 * p0 + b:4 * (p0 + z - a):4], A.add),
+                        tt(T.sn[:, C * b + p0:C * b + p0 + z - a], bank(4 * n + b, a, z), T.st[:, 4 * p0 + b:4 * (p0 + z - a):4], A.add,
                            ["B%d" % (4 * n + b), "sta%d" % h, "stb%d" % h], ["sn%d%d%d" % (b, h, m)])
         XN = T[xn]
 
         def back(q, b, h):
             out = XN[:, 4 * HF * h + b:4 * HF * (h + 1):4]
             win = T.sn[:, C * b:C * b + C].indirect(T.iu[:, (NS // 2) * h:(NS // 2) * (h + 1)])
-            reads = ["sn%d%d%d" % (b, h2, m) for h2 in range(2) for m in range(2)] + ["iu0", "iu1", "iu2"]
+            reads = ["sn%d%d%d" % (b, h2, m) for h2 in range(2) for m in range(2)] + ["iu"]
             if q == "S":
                 op("S", lambda: S.activation(out, win, F.Copy, scale=0.5), reads, [xn + "_%d%d" % (b, h)])
             else:

from concourse.bass import DstId, RemoteDMATransfer
from concourse.mybir import dt, AluOpType, ActivationFunctionType

C, R, N = 448, 2, 8
PC = C // N
HF = C // 2
NS = C // 16
SL = NS // 2
RW = 8 * SL
LAG = 2
CUTS = (0, 8, 14, 22, 28)
SUBS = ((0, 112), (112, 224), (224, 336), (336, 448))
BIG, LEAD = 2.0 ** 90, 32.0
HEAD = "m3 m2 f3 m1 f2 m0 f1 f0"
PLAN = ("ud e uc n ub ua u9 u8 u7 u6 u5 u4 u3 u2 u1 u0 s0 s1 s2 s3 c1 c0 d1 s4 d0 s5 s6 t00 t01 s7 s8 c2 g00 g01 s9 sa c3 d2 sb d3 "
        "sc sd r1 t10 t11 r0 g10 r2 g11 p0 p1 p2 p3")
SPLAN = [("w", s) for s in range(NS - 1, SL, -1)] + [("u", s) for s in range(SL, NS - 1)]
PAD = 128 - PC
X4, U8, BF, F32 = "float8_e4m3fn_x4", "uint8", "bfloat16", "float32"

SCRATCH = {
    "ps": ("psum", [128, 4096], F32),
    "ut": ("sbuf", [128, 512], BF), "vt": ("sbuf", [128, 512], BF),
    "qu": ("sbuf", [128, 128], X4), "su": ("sbuf", [128, 128], U8),
    "qp": ("sbuf", [128, 128], X4), "sp": ("sbuf", [128, 128], U8),
    "qv": ("sbuf", [128, 128], X4), "sv": ("sbuf", [128, 128], U8),
    "qw": ("sbuf", [128, 512], X4), "sw": ("sbuf", [128, 512], U8),
    "eighth": ("sbuf", [128, 512], BF), "ft": ("sbuf", [128, 2048], BF), "et": ("sbuf", [128, 2048], BF),
    "qf": ("sbuf", [128, 512], X4), "sf": ("sbuf", [128, 512], U8),
    "qe": ("sbuf", [128, 512], X4), "se": ("sbuf", [128, 512], U8),
    "pi": ("sbuf", [128, 8], "int32"), "pf": ("sbuf", [128, 16], F32),
    "ui": ("sbuf", [128, 8], "int32"), "uo": ("sbuf", [128, 8], "uint16"), "oo": ("sbuf", [128, 8], "uint16"),
    "t16": ("sbuf", [128, C], BF), "t32": ("sbuf", [128, 32], BF), "jv": ("sbuf", [128, C], BF),
    "jump": ("sbuf", [128, C], BF), "cap": ("sbuf", [128, C], BF), "keep": ("sbuf", [128, C], BF),
    "own": ("sbuf", [128, 256], BF), "k4": ("sbuf", [128, 12], F32), "k2": ("sbuf", [128, C], BF),
    "msk": ("sbuf", [128, C], F32), "fill": ("sbuf", [128, C], F32), "nc": ("sbuf", [128, C], BF),
    "f0": ("sbuf", [128, 8 * C], BF), "f1": ("sbuf", [128, 8 * C], BF), "so": ("sbuf", [128, SL * RW], "float16"),
    "sg": ("sbuf", [128, 8 * C], BF), "ac": ("sbuf", [128, 2 * NS], F32),
    "pb": ("sbuf", [128, 8 * (C + len(SUBS))], "float16"), "cs": ("sbuf", [128, C + 32], BF),
    "tu": ("sbuf", [128, 2 * C + 32], BF), "us": ("sbuf", [128, 2 * C + 32], BF),
    "rr": ("sbuf", [128, NS], F32), "r0": ("sbuf", [128, NS], F32), "r1": ("sbuf", [128, NS], F32), "r2": ("sbuf", [128, NS], F32),
    "iu": ("sbuf", [128, NS], "uint16"), "ob": ("sbuf", [128, C], BF), "ox": ("sbuf", [128, C], "float16"),
    "ou": ("sbuf", [128, C // 4], "uint16"), "olf": ("sbuf", [128, C], F32),
    "st": ("sbuf", [128, 4 * C], BF), "acc": ("sbuf", [128, 3 * PC], F32),
    "mt": ("sbuf", [128, 512], BF), "qm": ("sbuf", [128, 128], X4), "sm": ("sbuf", [128, 128], U8),
    "ht": ("sbuf", [128, 512], BF), "sn": ("sbuf", [128, 4 * C], F32), "yt": ("sbuf", [128, C], F32),
}
SEMAPHORES = ["cv", "cs", "cp", "cg", "du", "dxa", "dxb", "dw", "dv", "dout", "sent"]
for _t in range(R + 1):
    SCRATCH["x%d" % _t] = ("sbuf", [128, 4 * C], BF)
    SCRATCH["qx%d" % _t] = ("sbuf", [128, C], X4)
    SCRATCH["sx%d" % _t] = ("sbuf", [128, C], U8)
for _t in range(R):
    for _n, _w in (("s", C), ("l", C + PAD), ("g", C + PAD), ("r", 2 * PC), ("a", PC)):
        SCRATCH["q%s_%d" % (_n, _t)] = ("sbuf", [128, _w], X4)
        SCRATCH["s%s_%d" % (_n, _t)] = ("sbuf", [128, _w], U8)
    SEMAPHORES += [_s + str(_t) for _s in ("ra", "rb", "ga", "gb", "hr", "ha")]


def _bits(engines):
    return sum(1 << e for e in engines)


def _layout(T, topo):
    cores = list(T.cores)
    near0 = [r for r in range(N) if r == 0 or topo.may_write(cores[0], cores[r])]
    order = near0 + [r for r in range(N) if r not in near0]
    assert len(near0) == N // 2
    helpers = {}
    for k, r in enumerate(order):
        c = cores[r]
        far = [cores[order[j]] for j in range(N) if j // 4 != k // 4]
        cand = [h for h in topo.cores_of(c) if h != c and all(topo.may_write(h, d) for d in far)]
        same = [h for h in cand if topo.die(h) == topo.die(c)]
        other = [h for h in cand if topo.die(h) != topo.die(c)]
        helpers[r] = (other[:2], same[:2])
    return cores, order, helpers


def _xfer(topo, src, pairs, in_ap, engines, sem):
    ids = []
    for d, _ in pairs:
        rid, pid = topo.addr(d, src)
        ids.append(DstId(rid=rid, pnc=pid))
    if len(pairs) == 1:
        return RemoteDMATransfer(dst_ids=ids, dma_engine_mask=_bits(engines), remote_sem=sem, src=in_ap, dst=pairs[0][1])
    return RemoteDMATransfer(dst_ids=ids, dma_engine_mask=_bits(engines), remote_sem=sem, srcs=[in_ap],
                             dsts=[a for _, a in pairs])


def _slot(k, j):
    return PAD + PC * ((k - j) % 4 if k // 4 == j // 4 else 4 + k % 4)


def _view(T, kind, name, a, b):
    if kind == 0:
        return T["q" + name][:, a:b].bitcast(dt.uint8)
    return T["s" + name][:, a:b]


def _helper(g, core, T, topo, cores, order, r, kind, i):
    k = order.index(r)
    far = [j for j in range(N) if j // 4 != k // 4][2 * i:2 * i + 2]
    sent = 0
    for t in range(R):
        for src, wait, land, sem in (("r_%d", "hr", "l_%d", "rb"), ("a_%d", "ha", "g_%d", "gb")):
            g.wait_ge(T.sem[wait + str(t)], 8)
            xs = []
            for n, j in enumerate(far):
                d = cores[order[j]]
                e = topo.engines(core, d)
                half = len(e) // 2
                a = n * PC if wait == "hr" else 0
                xs.append(_xfer(topo, core, [(d, _view(T, kind, land % t, _slot(k, j), _slot(k, j) + PC))],
                                _view(T, kind, src % t, a, a + PC), e[n * half:(n + 1) * half], T.sem[sem + str(t)]))
                sent += half
            g.remote_dma_fused(xs, local_sem=T.sem.sent)
    g.wait_ge(T.sem.sent, sent)


def rank_program(g, core, T, topo):
    cores, order, helpers = _layout(T, topo)
    rank = T.rank_of(core)
    if rank is None:
        for r in range(N):
            for kind in (0, 1):
                if core in helpers[r][kind]:
                    _helper(g, core, T, topo, cores, order, r, kind, helpers[r][kind].index(core))
        return

    A, F = AluOpType, ActivationFunctionType
    V, S, P, Y = g.vector, g.scalar, g.tensor, g.sync
    Q = {"V": V, "S": S, "P": P, "G": g, "Y": Y}
    CNT = {"V": "cv", "S": "cs", "P": "cp", "G": "cg"}
    known = {q: {} for q in Q}
    total, waited, wr, rd = {}, {}, {}, {}

    def need(q, reads, writes, chain=False):
        evs = []
        for key in reads:
            evs += wr.get(key, [])
            if key[0] == "B":
                evs += [e for e in rd.get(key, []) if e[3] != q]
        for key in writes:
            evs += [e for e in wr.get(key, []) if not (chain and e[3] == q)] + rd.get(key, [])
        for sem, val, snap, _ in sorted(evs, key=lambda e: -e[1]):
            if known[q].get(sem, 0) < val:
                Q[q].wait_ge(T.sem[sem], val)
                waited[sem] = max(waited.get(sem, 0), val)
                known[q][sem] = val
            for s2, v2 in snap.items():
                if known[q].get(s2, 0) < v2:
                    known[q][s2] = v2

    def done(q, sem, n, reads, writes, tag):
        total[sem] = total.get(sem, 0) + n
        ev = (sem, total[sem], dict(known[q]), tag)
        for key in reads:
            rd.setdefault(key, []).append(ev)
        for key in writes:
            wr[key], rd[key] = [ev], []

    def op(q, fn, reads, writes, chain=False):
        need(q, reads, writes, chain)
        fn().then_inc(T.sem[CNT[q]], 1)
        done(q, CNT[q], 1, reads, writes, q)

    def dma(q, sem, pairs, reads, writes):
        need(q, reads, writes)
        for o, i in pairs:
            Q[q].dma_start(o, i).then_inc(T.sem[sem], 16)
        done(q, sem, 16 * len(pairs), [], writes, "D")

    def arrives(key, sem, n):
        total[sem] = n
        wr.setdefault(key, []).append((sem, n, {}, "D"))

    def send(xs, n, reads):
        need("G", reads, [])
        g.remote_dma_fused(xs, local_sem=T.sem.sent)
        total["sent"] = total.get("sent", 0) + n

    def bank(b, a, z):
        return T.ps[:, 512 * b + a:512 * b + z]

    def mm(b, lq, ls, l0, name, a, n, reads, start=True, stop=True):
        op("P", lambda: P.matmul_mx(bank(b, 0, n), lq[:, l0:l0 + 128], ls[:, l0:l0 + 128], T["q" + name][:, a:a + n],
                                    T["s" + name][:, a:a + n], start, stop), reads, ["B%d" % b], chain=not start)

    def quant(name, a, n, tile, reads, writes):
        op("V", lambda: V.quantize_mx(T["q" + name][:, a:a + n], T["s" + name][:, a:a + n], tile[:, 4 * a:4 * (a + n)]),
           reads, writes)

    def ts(out, in0, s1, s2, o0, o1, reads, writes):
        if o1 is None:
            op("V", lambda: V.tensor_scalar(out, in0, s1, None, o0), reads, writes)
        else:
            op("V", lambda: V.tensor_scalar(out, in0, s1, s2, o0, o1), reads, writes)

    def tt(out, in0, in1, o, reads, writes):
        op("V", lambda: V.tensor_tensor(out, in0, in1, o), reads, writes)

    def scan(out, d0, d1, first, o0, o1, reads, writes):
        op("V", lambda: V.tensor_tensor_scan(out, d0, d1, first, o0, o1), reads, writes)

    me = order.index(rank)
    mine, cross = me // 4, 1 - me // 4
    peers = [4 * mine + (me + d) % 4 for d in (1, 2, 3)]
    on = topo.engines(core, helpers[rank][0][0])
    off = topo.engines(core, cores[order[peers[0]]])
    rest = [e for e in on if e not in off]

    def flags(s, a, z):
        k = SL if s == NS else s % SL
        return T["f%d" % (k // 8)][:, 8 * a + k % 8:8 * z:8]

    dma("S", "du", [(T.ut[:], T.u[:])], [], ["ut"])
    dma("Y", "dxa", [(T.x0[:, 0:4 * HF], T.x[:, 0:4 * HF])], [], ["x0h0"])
    dma("Y", "dxb", [(T.x0[:, 4 * HF:4 * C], T.x[:, 4 * HF:4 * C])], [], ["x0h1"])
    small = dict(allow_small_or_imprecise_dtypes=True)
    op("G", lambda: g.iota(T.pi[:, 0:1], [[0, 1]], 0, 1), [], ["pi0"])
    op("G", lambda: g.iota(T.t32[:], [[1, 32]], 0, 0, **small), [], ["t32"])
    op("G", lambda: g.iota(T.ui[:], [[16, 8]], 0, 0), [], ["ui"])
    op("G", lambda: g.iota(T.t16[:], [[0, NS], [1, 16]], 0, 0, **small), [], ["t16"])
    op("G", lambda: g.iota(T.f1[:, 7:8 * C:8], [[0, C]], 0, 0, **small), [], ["z"])
    for s in range(SL):
        op("G", lambda: g.iota(flags(s, 16 * s, 16 * s + 16), [[0, 16]], 0, 0, **small), [], ["z%d" % s])
    op("G", lambda: g.iota(T.jv[:], [[1, C]], -HF, 0, **small), [], ["jv"])
    op("V", lambda: V.memset(T.eighth[:], 0.125), [], ["eighth"])
    ts(T.pi[:, 4:5], T.pi[:, 0:1], 4, 1, A.logical_shift_right, A.bitwise_and, ["pi0"], ["pi4"])
    ts(T.pi[:, 1:2], T.pi[:, 0:1], 15, None, A.bitwise_and, None, ["pi0"], ["pi1"])
    ts(T.pi[:, 2:3], T.pi[:, 0:1], 2, 3, A.logical_shift_right, A.bitwise_and, ["pi0"], ["pi2"])
    ts(T.pi[:, 3:4], T.pi[:, 0:1], 3, None, A.bitwise_and, None, ["pi0"], ["pi3"])
    op("V", lambda: V.memset(T.ac[:], 0.0), [], ["au%d" % s for s in range(NS)] + ["aw%d" % s for s in range(NS)])
    op("V", lambda: V.tensor_copy(T.pf[:, 0:5], T.pi[:, 0:5]), ["pi0", "pi1", "pi2", "pi3", "pi4"], ["pf"])
    op("V", lambda: V.tensor_copy(T.uo[:], T.ui[:]), ["ui"], ["uo"])
    ts(T.pf[:, 10:11], T.pf[:, 4:5], 512.0, -256.0, A.mult, A.add, ["pf"], ["pf10"])
    ts(T.pf[:, 11:12], T.pf[:, 4:5], -512.0 * 15.5, 256.0 * 15.5, A.mult, A.add, ["pf"], ["pf11"])
    op("S", lambda: S.activation(T.own[:, 0:32], T.t32[:], F.Sigmoid, bias=T.pf[:, 11:12], scale=T.pf[:, 10:11]),
       ["t32", "pf10", "pf11"], ["own"])
    ts(T.pf[:, 5:6], T.pf[:, 2:3], 0.0, 4.0, A.is_equal, A.mult, ["pf"], ["pf5"])
    ts(T.pf[:, 8:9], T.pf[:, 1:2], float(PC * (me % 4) - PAD), None, A.add, None, ["pf"], ["pf8"])
    ts(T.pf[:, 9:10], T.pf[:, 1:2], 0.25, None, A.add, None, ["pf"], ["pf9"])
    ts(T.pf[:, 12:13], T.pf[:, 5:6], T.pf[:, 2:3], -1.0, A.add, A.add, ["pf", "pf5"], ["pf12"])
    ts(T.pf[:, 6:7], T.pf[:, 5:6], 2.0 * C, T.pf[:, 3:4], A.mult, A.add, ["pf", "pf5"], ["pf6"])
    ts(T.k4[:, 0:4], T.t32[:, 0:4], T.pf[:, 2:3], 1.0 * C, A.is_equal, A.mult, ["pf", "t32"], ["ka"])
    ts(T.k4[:, 4:8], T.t32[:, 0:4], T.pf[:, 12:13], -2.0 * C, A.is_equal, A.mult, ["pf12", "t32"], ["kb"])
    op("V", lambda: V.memset(T.cs[:], 0.0), [], ["cs%d" % n for n in range(len(SUBS))])
    op("V", lambda: V.memset(T.ob[:], 0.0), [], ["ob"])
    ts(T.jump[:], T.t16[:], T.pf[:, 1:2], 2 * BIG, A.is_equal, A.mult, ["pf", "t16"], ["jump"])
    tt(T.k4[:, 8:12], T.k4[:, 0:4], T.k4[:, 4:8], A.add, ["ka", "kb"], ["k4"])
    ts(T.keep[:], T.t16[:], 0.0, None, A.not_equal, None, ["t16"], ["keep"])
    quant("u", 0, 128, T.ut, ["ut"], ["qu"])
    ts(T.cap[:], T.jump[:], -1.0, BIG, A.mult, A.add, ["jump"], ["cap"])
    op("V", lambda: V.tensor_copy(T.qp[:].bitcast(dt.uint32), T.qu[:].bitcast(dt.uint32).indirect(T.uo[:, 0:8])),
       ["qu", "uo"], ["qp"])
    op("S", lambda: S.activation(T.sp[:], T.su[:].indirect(T.uo[:, 0:8]), F.Copy), ["qu", "uo"], ["sp"])
    ts(T.jump[:, 0:C:16], T.t16[:, 0:NS], 0.0, 2 * BIG, A.mult, A.add, ["t16"], ["jump"])
    quant("x0", 0, HF, T.x0, ["x0h0"], ["qx0h0"])
    quant("x0", HF, HF, T.x0, ["x0h1"], ["qx0h1"])
    ts(T.pf[:, 7:8], T.pf[:, 6:7], -4.0 * HF, None, A.add, None, ["pf6"], ["pf7"])
    ts(T.oo[:], T.ui[:], T.pf[:, 8:9], 0.0, A.add, A.max, ["ui", "pf8"], ["oo"])
    for n, (a, z) in enumerate(SUBS):
        ts(T.pb[:, 8 * (a + n):8 * (a + n + 1)], T.t32[:, 0:8], 0.0, LEAD, A.mult, A.add, ["t32"], ["lead%d" % n])
    for b in range(4):
        if b < 3:
            n = 32 << b
            op("S", lambda: S.activation(T.own[:, n:2 * n], T.own[:, 0:n], F.Copy), ["own"], ["own"])
        op("S", lambda: S.activation(T.k2[:, b:C:4], T.t16[:, 0:C // 4], F.Identity, bias=T.k4[:, 8 + b:9 + b], scale=0.0),
           ["k4", "t16"], ["k2%d" % b])
    for b in range(4):
        op("G", lambda: g.affine_select(T.ft[:, 512 * b:512 * b + 512], T.eighth[:], [[-1, 512]], A.is_equal, 0.0, b, 4),
           ["eighth"], ["ft%d" % b])
    dma("Y", "dw", [(T.qw[:].bitcast(dt.uint8), T.wc[:]), (T.sw[:], T.ws[:])], ["x0h1"], ["qw"])
    dma("Y", "dv", [(T.vt[:], T.v[:])], [], ["vt"])

    up = {s: (16 * s + 16, min(C, 16 * (s + 1 + (SL if s < SL else SL - 1)))) for s in range(NS - 1)}
    wrap = {s: (0, 16 * (s - SL)) for s in range(SL + 1, NS)}

    for t in range(R):
        xk, xn = "x%d" % t, "x%d" % (t + 1)
        xkeys = [xk + "h0", xk + "h1"] if t == 0 else [xk + "_%d%d" % (b, h) for b in range(4) for h in range(2)]
        for b in range(2):
            mm(b, T.qp, T.sp, 0, xk, 0, C, ["qp", "sp", "q" + xk + "h0", "q" + xk + "h1"])

        def msk(n):
            a, z = 16 * CUTS[n], 16 * CUTS[n + 1]
            tt(T.msk[:, a:z], bank(0, a, z), T.cap[:, a:z], A.max, ["B0", "cap"], ["msk%d" % n])

        def fill(n):
            a, z = 16 * CUTS[n], 16 * CUTS[n + 1]
            scan(T.fill[:, a:z], T.jump[:, a:z], T.msk[:, a:z], 0.0, A.add, A.min, ["jump", "msk%d" % n], ["fill%d" % n])

        def zc(s):
            return T.fill[:, 16 * s + 15:16 * s + 16]

        def zk(s):
            return "fill%d" % max(n for n in range(len(CUTS) - 1) if CUTS[n] <= s)

        for w in HEAD.split():
            (msk if w[0] == "m" else fill)(int(w[1]))
        at = [0]

        def sign(n):
            k, s = SPLAN[n]
            a, z = (up if k == "u" else wrap)[s]
            at.append(at[-1] + z - a)
            op("S", lambda: S.activation(T.sg[:, at[n]:at[n + 1]], bank(1, a, z), F.Sign, bias=zc(s), scale=-1.0),
               ["B1", zk(s)], ["sg%d" % n])

        def flag(n):
            k, s = SPLAN[n]
            a, z = (up if k == "u" else wrap)[s]
            src = T.sg[:, at[n]:at[n + 1]]
            if k == "u":
                op("S", lambda: S.activation(flags(s, a, z), src, F.Relu, scale=-1.0, accum_out=T.ac[:, s:s + 1]),
                   ["sg%d" % n], ["Fu%d" % s, "au%d" % s])
            else:
                op("S", lambda: S.activation(flags(s, a, z), src, F.Sigmoid, bias=128.0, scale=-256.0,
                                             accum_out=T.ac[:, NS + s:NS + s + 1]), ["sg%d" % n], ["Fw%d" % s, "aw%d" % s])

        for n in range(len(SPLAN) + LAG):
            if n < len(SPLAN):
                sign(n)
            if n >= LAG:
                flag(n - LAG)

        def row(s):
            a, z = up[s]
            ts(flags(s, a, z), bank(0, a, z), zc(s), None, A.is_gt, None, ["B0", zk(s)], ["Fu%d" % s])

        def inside():
            tt(flags(NS, 0, C), bank(0, 0, C), T.fill[:], A.is_gt, ["B0"] + ["fill%d" % n for n in range(len(CUTS) - 1)], ["D"])

        def inrow():
            scan(T.nc[:], T.keep[:], flags(NS, 0, C), 0.0, A.mult, A.add, ["keep", "D"], ["nc"])

        def rsum(s):
            a, z = up[s]
            m = (a + z) // 2
            scan(T.so[:, s * RW:(s + 1) * RW], flags(s, a, m), flags(s, m, z), T.nc[:, 16 * s + 15:16 * s + 16], A.add, A.add,
                 ["Fu%d" % s, "nc"], ["so%d" % s])

        def col(n):
            a, z = SUBS[n]
            keys = ["Fu%d" % s for s in up if up[s][0] < z and up[s][1] > a] + ["Fw%d" % s for s in wrap if wrap[s][1] > a]
            scan(T.pb[:, 8 * (a + n + 1):8 * (z + n + 1)], T.f0[:, 8 * a:8 * z], T.f1[:, 8 * a:8 * z], LEAD, A.add, A.add,
                 keys + ["D", "z"] + ["z%d" % s for s in range(SL)], ["pb%d" % n])

        def diff(n):
            a, z = SUBS[n]
            scan(T.cs[:, 16 + a:16 + z], T.pb[:, 8 * (a + n + 1) + 7:8 * (z + n + 1):8], T.pb[:, 8 * (a + n) + 7:8 * (z + n):8],
                 0.0, A.max, A.subtract, ["pb%d" % n, "lead%d" % n], ["cs%d" % n])

        def piece(c, w):
            return (16 + HF * c, HF, HF * c) if w == 0 else (HF * c, HF + 32 * c, C + HF * c)

        def turn(c, w):
            a, n, o0 = piece(c, w)
            keys = ["cs%d" % k for k in range(len(SUBS)) if SUBS[k][0] + 16 < a + n and SUBS[k][1] + 16 > a]
            op("V", lambda: V.transpose(T.tu[:, o0:o0 + n], T.cs[:, a:a + n]), keys, ["tu%d%d" % (c, w)])

        def gsum(c, w):
            a, n, o0 = piece(c, w)
            scan(T.us[:, o0:o0 + n], T.tu[:, o0:o0 + n], T.own[:, 0:n], 0.0, A.add, A.mult, ["tu%d%d" % (c, w), "own"], ["us%d%d" % (c, w)])

        def rows(w):
            if w == 0:
                ts(T.rr[:, 0:SL], T.so[:, RW - 1:SL * RW:RW], -16.0, None, A.add, None, ["so%d" % s for s in range(SL)], ["rr0"])
            elif w == 1:
                tt(T.r0[:, SL:NS], T.ac[:, NS + SL:2 * NS], T.nc[:, HF + 15:C:16], A.add,
                   ["nc"] + ["aw%d" % s for s in range(SL, NS)], ["rs"])
            else:
                tt(T.rr[:, SL:NS], T.r0[:, SL:NS], T.ac[:, SL:NS], A.add, ["rs"] + ["au%d" % s for s in range(SL, NS)], ["rr1"])

        def place(w):
            if w == 0:
                tt(T.r1[:], T.rr[:], T.us[:, 15:C:16], A.subtract, ["rr0", "rr1", "us00", "us10"], ["r1"])
            elif w == 1:
                tt(T.r2[:], T.r1[:], T.us[:, C + 31:2 * C + 16:16], A.subtract, ["r1", "us01", "us11"], ["r2"])
            elif w == 2:
                ts(T.iu[:], T.r2[:], T.pf[:, 9:10], 16.0 * SL, A.add, A.add, ["r2", "pf9"], ["iu"])
            else:
                op("V", lambda: V.tensor_copy(T.ob[:, 0:C].indirect(T.iu[:, 0:NS]), T.jv[:]), ["iu", "jv"], ["ob"])

        calls = {"u": row, "e": inside, "n": inrow, "c": col, "d": diff, "t": turn, "g": gsum, "r": rows, "p": place, "s": rsum}
        for w in PLAN.split():
            calls[w[0]](*[int(ch, 16) for ch in w[1:]])
        scan(T.ox[:], T.ob[:], T.k2[:], -1000.0, A.max, A.add, ["ob", "k20", "k21", "k22", "k23"], ["ox"])
        ts(T.ou[:], T.ox[:, 3:C:4], 4.0, T.pf[:, 7:8], A.mult, A.add, ["ox", "pf7"], ["ou"])

        X = T[xk]
        sk, lk, gk, rk, ak = ["%s_%d" % (n, t) for n in "slgra"]
        for h, cut in ((cross, 28), (mine, 22)):
            o0 = PC * h
            op("S", lambda: S.activation(T.st[:, 16 * (o0 + cut):16 * (o0 + PC)], X[:, 0:4 * C].indirect(T.ou[:, o0 + cut:o0 + PC]), F.Copy),
               ["ou"] + xkeys, ["stb%d" % h])
            op("V", lambda: V.tensor_copy(T.st[:, 16 * o0:16 * (o0 + cut)], X[:, 0:4 * C].indirect(T.ou[:, o0:o0 + cut])),
               ["ou"] + xkeys, ["sta%d" % h])
            quant(sk, HF * h, HF, T.st, ["sta%d" % h, "stb%d" % h], ["q%sh%d" % (sk, h)])
            if h == cross:
                for kind in (0, 1):
                    xs = []
                    for i, hc in enumerate(helpers[rank][kind]):
                        a = HF * h + 2 * PC * i
                        xs.append(_xfer(topo, core, [(hc, _view(T, kind, rk, 0, 2 * PC))], _view(T, kind, sk, a, a + 2 * PC),
                                        on[i::2], T.sem["hr%d" % t]))
                    send(xs, len(on), ["q%sh%d" % (sk, h)])
            else:
                q4 = len(off) // 4
                share = ((off[:2 * q4], off[2 * q4:3 * q4], off[3 * q4:]), (off[2 * q4:], off[:q4], off[q4:2 * q4]))
                for kind in (0, 1):
                    xs = [_xfer(topo, core, [(cores[order[j]], _view(T, kind, lk, _slot(me, j), _slot(me, j) + PC))],
                                _view(T, kind, sk, j * PC, j * PC + PC), share[kind][n], T.sem["ra%d" % t])
                          for n, j in enumerate(peers)]
                    send(xs, len(off), ["q%sh%d" % (sk, h)])
                op("V", lambda: V.tensor_copy(T["q" + lk][:, 0:128].bitcast(dt.uint32),
                                              T["q" + sk][:, HF * h:HF * h + HF].bitcast(dt.uint32).indirect(T.oo[:, 0:8])),
                   ["q%sh%d" % (sk, h), "oo"], [lk + "q"])
                op("S", lambda: S.activation(T["s" + lk][:, 0:128], T["s" + sk][:, HF * h:HF * h + HF].indirect(T.oo[:, 0:8]), F.Copy),
                   ["q%sh%d" % (sk, h), "oo"], [lk + "s"])
        arrives(lk + "h%d" % mine, "ra%d" % t, 2 * len(off))
        arrives(lk + "h%d" % cross, "rb%d" % t, 4 * len(off))

        if t == 0:
            fk = ["ft%d" % b for b in range(4)]
            op("S", lambda: S.activation(T.et[:], T.ft[:], F.Copy, scale=8.0), fk, ["et"])
            quant("f", 0, 512, T.ft, fk, ["qf"])
            op("V", lambda: V.memset(T.mt[:], 0.0), [], ["mt0", "mt1", "mt2", "mt3"])
            op("V", lambda: V.memset(T.ht[:], 0.0), [], ["ht0", "ht1", "ht2", "ht3"])
            quant("v", 0, 128, T.vt, ["vt"], ["qv"])
            quant("e", 0, 512, T.et, ["et"], ["qe"])
        if t == R - 1:
            ts(T.olf[:], T.ob[:], 1.0 * HF, None, A.add, None, ["ob"], ["olf"])
            dma("Y", "dout", [(T.ol[k:k + 1, :], T.olf[16 * k:16 * k + 1, :]) for k in range(8)],
                ["olf", lk + "h%d" % mine], [])

        for h in (mine, cross):
            for b in range(3):
                mm((2 if h == mine else 5) + b, T.qf, T.sf, 128 * b, lk, PAD + (0 if h == mine else HF), HF,
                   ["qf", lk + "h%d" % h, lk + "q", lk + "s"])
        for r in range(N):
            mm(0, T.qf, T.sf, 128 * 3, lk, _slot(order.index(r), me) - PAD, 128, ["qf", lk + "h0", lk + "h1"], r == 0, r == N - 1)
        seq = list(range(N))
        if order.index(0) // 4 != mine and order.index(1) // 4 == mine:
            seq[0], seq[1] = 1, 0
        for n, r in enumerate(seq):
            k = order.index(r)
            for b in range(3):
                bk = (2 if k // 4 == mine else 5) + b
                a = (_slot(k, me) - PAD) % HF
                src, acc = bank(bk, a, a + PC), T.acc[:, b * PC:b * PC + PC]
                if n == 0:
                    op("V", lambda: V.tensor_copy(acc, src), ["B%d" % bk], ["acc%d" % b])
                elif n < N - 1:
                    tt(acc, src, acc, A.add, ["B%d" % bk], ["acc%d" % b])
                else:
                    tt(T.mt[:, 4 * PAD + b:512:4], src, acc, A.add, ["B%d" % bk, "acc%d" % b], ["mt%d" % b])
        op("S", lambda: S.activation(T.mt[:, 4 * PAD + 3:512:4], bank(0, PAD, 128), F.Copy), ["B0"], ["mt3"])
        quant("m", 0, 128, T.mt, ["mt0", "mt1", "mt2", "mt3"], ["qm"])
        for b in range(4):
            mm(b, T.qw, T.sw, 128 * b, "m", 0, 128, ["qw", "qm"])
        for b in range(4):
            if b % 2 == 0:
                op("S", lambda: S.activation(T.ht[:, 4 * PAD + b:512:4], bank(b, PAD, 128), F.Relu, scale=0.0625), ["B%d" % b], ["ht%d" % b])
            else:
                ts(T.ht[:, 4 * PAD + b:512:4], bank(b, PAD, 128), 0.0, 0.0625, A.max, A.mult, ["B%d" % b], ["ht%d" % b])
        quant(gk, 0, 128, T.ht, ["ht0", "ht1", "ht2", "ht3"], [gk + "q"])

        for kind in (0, 1):
            src = _view(T, kind, gk, PAD, 128)
            send([_xfer(topo, core, [(hc, _view(T, kind, ak, 0, PC)) for hc in helpers[rank][kind]], src, rest, T.sem["ha%d" % t]),
                  _xfer(topo, core, [(cores[order[j]], _view(T, kind, gk, _slot(me, j), _slot(me, j) + PC)) for j in peers], src, off,
                        T.sem["ga%d" % t])], len(on), [gk + "q"])
        arrives(gk + "h%d" % mine, "ga%d" % t, 6 * len(off))
        arrives(gk + "h%d" % cross, "gb%d" % t, 4 * len(off))

        for n, h in enumerate((mine, cross)):
            for b in range(4):
                mm(4 * n + b, T.qe, T.se, 128 * b, gk, PAD + HF * n, HF, ["qe", gk + "q", gk + "h%d" % h])
        for n, h in enumerate((mine, cross)):
            rot = PC * (me % 4) if n == 0 else 0
            for b in range(4):
                for m, (a, z, p0) in enumerate(((0, HF - rot, HF * h + rot), (HF - rot, HF, HF * h))):
                    if z > a:
                        tt(T.sn[:, C * b + p0:C * b + p0 + z - a], bank(4 * n + b, a, z), T.st[:, 4 * p0 + b:4 * (p0 + z - a):4], A.add,
                           ["B%d" % (4 * n + b), "sta%d" % h, "stb%d" % h], ["sn%d%d%d" % (b, h, m)])
        XN = T[xn]

        def back(q, b, h):
            out = XN[:, 4 * HF * h + b:4 * HF * (h + 1):4]
            win = T.sn[:, C * b:C * b + C].indirect(T.iu[:, (NS // 2) * h:(NS // 2) * (h + 1)])
            reads = ["sn%d%d%d" % (b, h2, m) for h2 in range(2) for m in range(2)] + ["iu"]
            if q == "S":
                op("S", lambda: S.activation(out, win, F.Copy, scale=0.5), reads, [xn + "_%d%d" % (b, h)])
            else:
                ts(out, win, 0.5, None, A.mult, None, reads, [xn + "_%d%d" % (b, h)])

        for b, h in ((0, 0), (1, 0), (0, 1), (1, 1), (2, 1)):
            back("S", b, h)
        back("V", 2, 0)
        back("V", 3, 0)
        quant(xn, 0, HF, XN, [xn + "_%d0" % b for b in range(4)], ["q" + xn + "h0"])
        back("V", 3, 1)
        quant(xn, HF, HF, XN, [xn + "_%d1" % b for b in range(4)], ["q" + xn + "h1"])

    xk = "x%d" % R
    for h in range(2):
        a, z = HF * h, HF * h + HF
        mm(h, T.qv, T.sv, 0, xk, a, HF, ["qv", "q%sh%d" % (xk, h)])
        dma("Y", "dout", [(T.oc[:, 4 * a:4 * z], _view(T, 0, xk, a, z))], ["q%sh%d" % (xk, h)], [])
        if h == 0:
            op("S", lambda: S.activation(T.yt[:, a:z], bank(h, 0, HF), F.Copy), ["B%d" % h], ["yt%d" % h])
        else:
            op("V", lambda: V.tensor_copy(T.yt[:, a:z], bank(h, 0, HF)), ["B%d" % h], ["yt%d" % h])
        dma("S", "dout", [(T.y[:, a:z], T.yt[:, a:z])], ["yt%d" % h], [])
    dma("Y", "dout", [(T.osc[4 * k:4 * k + 4, :], T["s" + xk][32 * k:32 * k + 4, :]) for k in range(4)],
        ["q%sh0" % xk, "q%sh1" % xk], [])
    for sem, n in total.items():
        if waited.get(sem, 0) < n:
            g.wait_ge(T.sem[sem], n)
